import numpy as np, ml_dtypes
CORES = [40,64,80,88,96,104,120,144]
N = 8
BF = ml_dtypes.bfloat16
def gentries(a):
    return np.ascontiguousarray(a.reshape(8, 16, -1).transpose(0, 2, 1)).reshape(8, -1)
def gtable(e):
    e = np.asarray(e); return np.ascontiguousarray(e.reshape(8, -1, 16).transpose(0, 2, 1)).reshape(128, -1).astype(np.int32)
W, UM, O, T, ST = 4096, 4096, 192, 4, 5
def parts(rng):
    x = rng.integers(0, 256, (N, 128, W), dtype=np.int16)
    p = rng.integers(0, W, (N, 8, W)); v = rng.integers(0, W, (N, 8, O, 16)); y = rng.integers(0, 256, (N, 128, O)); w = rng.integers(0, 256, (N, 128, 1))
    lm = np.zeros((N, 8, 2), np.int64)
    for q in range(N):
        lm[q, :, 0] = rng.permutation(np.array([400, 1000, 1150, 1300, 1400, 1550, 1700, 2600])) + rng.integers(-50, 51, 8)
        lm[q, :, 1] = rng.permutation(np.array([1100, 1200, 1300, 1400, 1500, 1600, 1700, 1800])) + rng.integers(-50, 51, 8)
    return x, p, v, y, w, lm
def pack(x, p, v, y, w, lm):
    return {"claim": np.ascontiguousarray(x).astype(np.float32).astype(BF), "par": np.ascontiguousarray(p).astype(np.int32), "who": np.stack([gtable(a.reshape(8, -1)) for a in v]),
            "est": np.ascontiguousarray(y).astype(np.float32).astype(BF), "wt": np.ascontiguousarray(w).astype(np.int32), "lim": np.ascontiguousarray(lm).astype(np.int32)}
def setup_inputs(rng):
    return pack(*parts(rng))
def setup_inputs_spread(rng):
    x, p, v, y, w, lm = parts(rng)
    x = (x.reshape(N, 8, 16, W) >> rng.integers(0, 9, (N, 8, 1, W)).astype(np.int16)).reshape(N, 128, W)
    p = np.minimum((W * rng.random(p.shape) ** 2).astype(np.int64), W - 1); v = np.minimum((W * rng.random(v.shape) ** 3).astype(np.int64), W - 1)
    y = (y.reshape(N, 8, 16, O) >> rng.integers(0, 9, (N, 8, 1, O))).reshape(N, 128, O); w = w >> rng.integers(0, 8, w.shape)
    lm = np.minimum(np.exp2(5 + 7 * rng.random(lm.shape)).astype(np.int64), 4080)
    return pack(x, p, v, y, w, lm)
def setup_inputs_ends(rng):
    c = rng.integers(0, 4, (N, 8, 1, W), dtype=np.int16); x = (255 * np.where(c < 2, c, rng.integers(0, 2, (N, 8, 16, W), dtype=np.int16))).reshape(N, 128, W)
    p = (W - 1) * rng.integers(0, 2, (N, 8, W))
    v = np.where(rng.random((N, 8, O, 1)) < 0.2, rng.integers(0, W, (N, 8, O, 16)), (W - 1) * rng.integers(0, 2, (N, 8, O, 16)))
    c = rng.integers(0, 4, (N, 8, 1, O)); y = (255 * np.where(c < 2, c, rng.integers(0, 2, (N, 8, 16, O)))).reshape(N, 128, O)
    w = 255 * rng.integers(0, 2, (N, 8, 16)); w[:, 3] = 0; w[:, 7] = 255; w = w.reshape(N, 128, 1)
    lm = np.full((N, 8, 2), 4080, np.int64)
    for q in range(N):
        for b in range(2): lm[q, :7, b] = 4080 * rng.permutation(np.array([0, 0, 0, 0, 1, 1, 1]))
    u = (16 * 255 * 255) & (UM - 1); hl = ((((W - 1) * u) >> 5) + W - 1) & (W - 1); h1 = ((u >> 5) + 1) & (W - 1)
    x[:, 112:, 0] = 0; x[:, 112:, hl] = 255; x[:, 112:, h1] = 255
    p[:, 7, 0] = W - 1; p[:, 7, 1] = 0; p[:, 7, W - 1] = 0
    y[:, 112:, O - 1] = 255; y[:, 112:, 3] = 255
    v[:, 7, O - 1] = 0; v[:, 7, O - 1, 14] = W - 1; v[:, 7, O - 1, 15] = 1
    v[:, 7, 3] = 0; v[:, 7, 3, 1] = W - 1; v[:, 7, 3, 2] = W - 1
    return pack(x, p, v, y, w, lm)
def setup_inputs_corners(rng):
    x, p, v, y, w, lm = parts(rng); sh = int(rng.integers(0, 8)); a = np.arange(W)
    for q in range(N):
        for g in range(8):
            m = (g + q + sh) % 8; lo, hi = 16 * g, 16 * g + 16
            if m == 0:
                p[q, g] = np.minimum(a + 1, W - 1); lm[q, g] = (4080, 1500); v[q, g, 0] = W - 1; v[q, g, 1] = 0; v[q, g, O - 1, 15] = W - 2
            elif m == 1:
                p[q, g] = a; lm[q, g] = (1, 0)
            elif m == 2:
                p[q, g] = 0; lm[q, g] = (0, 0); v[q, g] = rng.integers(0, W, (O, 1)); v[q, g, ::2] = W - 1
            elif m == 3:
                pool = np.concatenate([np.array([0, W - 1]), 1 + rng.permutation(W - 2)[:6]]); v[q, g] = pool[rng.integers(0, 8, (O, 16))]; p[q, g] = W - 1; lm[q, g] = (1300, 0)
            elif m == 4:
                w[q, lo:hi] = 0; lm[q, g] = (1, 0)
                e = rng.permutation(W)[:19]; c = x[q, lo:hi]
                c[:, e[:16]] = 255; c[np.arange(14), e[1:15]] = 0; c[14:, e[15]] = 0
                c[:, e[16:18]] = 0; c[:, e[18]] = 127
                p[q, g, e[:16]] = e[16]; p[q, g, e[16:18]] = e[1]; p[q, g, e[18]] = e[18]
                v[q, g, O - 1] = e[:16]
                v[q, g, O - 2] = e[:16]; v[q, g, O - 2, 0] = e[18]
                v[q, g, 0] = e[16]; v[q, g, 0, 0] = e[0]; v[q, g, O - 3] = e[17]; v[q, g, O - 3, 0] = e[0]
            elif m == 5:
                w[q, lo:hi] = 255; y[q, lo:hi] = 255; lm[q, g] = (1300, 4080)
            elif m == 6:
                v[q, g] = rng.permutation(W)[:16 * O].reshape(O, 16); lm[q, g] = (1200, 0)
            else:
                p[q, g] = W - 1 - a; w[q, lo:hi] = 0; w[q, lo + int(rng.integers(0, 16))] = 1; y[q, lo:hi, 0] = 0; lm[q, g] = (4080, 0)
    return pack(x, p, v, y, w, lm)
def setup_inputs_counts(rng):
    x, p, v, y, w, lm = parts(rng); a = int(rng.integers(0, N)); b = (a - ST) % N; d = (a - 2 * ST) % N; s = np.arange(W)
    p[d, :, :64] = np.arange(64); v[d] = rng.integers(0, 63, (8, O, 16)); lm[d, :, 0] = 1360 + rng.integers(-50, 51, 8)
    lm[b, :, 0] = 0; v[b] = rng.integers(64, W, (8, O, 16))
    w[a] = 0; x[a] = (x[a] & 63) + 191 * (s & 1)
    p[a] = (p[a] - (p[a] & 1)) + ((s + (s >= 64)) & 1); p[a, :, 63] = 63
    lm[a, :, 0] = 340 + rng.integers(-20, 21, 8); lm[a, :, 1] = 4080
    v[a] = rng.integers(64, W, (8, O, 16)); v[a, 7, O - 1] = 63; v[a, 0, 0, :15] = 63
    return pack(x, p, v, y, w, lm)
def setup_inputs_ties(rng):
    x, p, v, y, w, lm = parts(rng)
    z = np.stack([rng.permutation(np.array([1, 1, 3, 3, 8, 31, 64, 85])) for q in range(N)])
    x = ((x & 3).reshape(N, 8, 16, W) * z[:, :, None, None]).reshape(N, 128, W)
    lm = np.stack([z * rng.integers(17, 23, (N, 8)), z * rng.integers(18, 27, (N, 8))], axis=2)
    v[:, ::3] = v[:, ::3] & 63
    return pack(x, p, v, y, w, lm)
def check_inputs(d):
    bad = []
    for k, lo, hi in (("claim", 0, 255), ("par", 0, W - 1), ("who", 0, W - 1), ("est", 0, 255), ("wt", 0, 255), ("lim", 0, 4080)):
        a = np.asarray(d[k]).astype(np.float32)
        if not (np.min(a) >= lo and np.max(a) <= hi): bad.append("range of " + k)
        elif not np.all(np.floor(a) == a): bad.append("whole numbers of " + k)
    return bad
def place(s, u, t):
    return (((s * u[:, :, None]) >> 5) + s + 77 * t) & (W - 1)
def reference(claim, par, who, est, wt, lim):
    X = np.ascontiguousarray(np.asarray(claim).astype(np.float32).astype(np.int32).reshape(N, 8, 16, W).transpose(0, 1, 3, 2))
    P = np.asarray(par).astype(np.int64); V = np.stack([gentries(a) for a in who]).astype(np.int64).reshape(N, 8, O, 16)
    Y = np.ascontiguousarray(np.asarray(est).astype(np.float32).astype(np.int64).reshape(N, 8, 16, O).transpose(0, 1, 3, 2))
    wq = np.asarray(wt).astype(np.int64).reshape(N, 8, 1, 16); lm = np.asarray(lim).astype(np.int64)
    G = np.arange(8)[:, None]; cnt = [0] * N
    for t in range(T):
        for q in range(N):
            r = (q - ST * t) % N; v = V[r]; y0 = Y[r]
            u = np.add.reduce(wq[q] * y0, axis=2) & (UM - 1)
            p = P[q][G, v.reshape(8, -1)].reshape(8, O, 16)
            x = X[q][G, place(v, u, t).reshape(8, -1)].reshape(8, O, 16, 16)
            z = X[q][G, place(p, u, t).reshape(8, -1)].reshape(8, O, 16, 16)
            dep = np.add.reduce(np.abs(x - z), axis=3) < lm[q, :, 0][:, None, None] + cnt[q]
            cand = ~dep | np.all(dep, axis=2, keepdims=True)
            M = (np.max(np.where(cand[..., None], x, -1), axis=2) + np.min(np.where(cand[..., None], x, 256), axis=2)) >> 1
            far = np.where(cand, np.add.reduce(np.abs(x - M[:, :, None, :]), axis=3), 1 << 20)
            y = np.take_along_axis(x, np.argmin(far, axis=2)[:, :, None, None], 2)[:, :, 0, :]
            err = np.add.reduce(np.abs(x - y[:, :, None, :]), axis=3)
            j = np.argmax(err, axis=2)[:, :, None]; rest = np.where(np.arange(16) == j, -1, err); k = np.argmax(rest, axis=2)[:, :, None]
            ask = np.take_along_axis(rest, k, 2)[:, :, 0] >= lm[q, :, 1][:, None]
            vj = np.take_along_axis(v, j, 2)[:, :, 0]; vk = np.take_along_axis(v, k, 2)[:, :, 0]
            for g in range(8):
                o = np.nonzero(ask[g])[0]
                if len(o):
                    s, first = np.unique(vk[g, o], return_index=True)
                    P[q, g, s] = vj[g, o[first]]
            V[r] = np.where(dep, p, v); Y[r] = (y0 + y) >> 1
            cnt[q] = int(np.count_nonzero(dep)) & 31
    return {"yv": np.stack([gtable(a.reshape(8, -1)) for a in V]).astype(np.float32), "ye": np.ascontiguousarray(Y.transpose(0, 1, 3, 2)).reshape(N, 128, O).astype(np.float32).astype(BF), "yp": P.astype(np.float32)}

@@ -1,0 +1,620 @@
+import numpy as np
+import comms_topo
+from concourse.mybir import dt, AluOpType, AxisListType, ActivationFunctionType
+
+OP = AluOpType
+AF = ActivationFunctionType
+NV, NC, STEP = 4, 96, 5
+CW = 8432
+
+TILES = {}
+SIZE = {"bf": 0, "f": 0, "i": 0, "u": 0}
+_al = {"bf": 16, "f": 8, "i": 8, "u": 16}
+
+
+def _tile(kind, name, n):
+    TILES[name] = (kind, SIZE[kind], n)
+    a = _al[kind]
+    SIZE[kind] += (n + a - 1) // a * a
+
+
+for _p in range(2):
+    for _c in range(2):
+        _s = "%d%d" % (_p, _c)
+        for _n, _w in (("X", 1536), ("PR", 1536), ("D", 1536), ("A", 1536), ("S1", 512 * 3), ("S2", 512 * 3), ("DEP", 96), ("CAN", 96),
+                       ("MT", 128), ("YG", 96), ("YT", 128), ("G", 192), ("EE", 576), ("DAT", 96), ("YB", 96)):
+            _tile("bf", _n + _s, _w)
+        for _n, _w in (("UP", 96), ("VF", 96), ("UH", 96), ("DV", 96), ("VT", 96), ("VN", 96), ("M", 96), ("MM", 192), ("W", 96), ("ASK", 8),
+                       ("AW", 8), ("R", 96), ("RS", 96), ("TT", 8), ("WN", 8), ("LS", 8), ("L2", 8), ("S12", 8)):
+            _tile("f", _n + _s, _w)
+        for _n, _w in (("UI", 96), ("UJ", 96), ("T1", 96), ("T2", 96), ("T3", 96), ("Q1", 96), ("Q2", 96), ("Q3", 96), ("I1", 8), ("I2", 8),
+                       ("YS", 96), ("YH", 96), ("E1", 16), ("E2", 16)):
+            _tile("i", _n + _s, _w)
+        for _n, _w in (("XL", 96), ("ZL", 96), ("VL", 96), ("YL", 16), ("AB", 16), ("SL", 16)):
+            _tile("u", _n + _s, _w)
+for _n, _w in (("I128", 128), ("TL", 128), ("TI", 128), ("BD", 128), ("WBD", 128), ("BV", 128), ("SUM", 2048), ("WTL", 2048), ("PEX", 2048),
+               ("VEX", 2048), ("EXP", 2048), ("ONE", 128), ("HALF", 1536), ("EM0", 1536), ("EM1", 1536), ("EY0", 1536), ("EY1", 1536), ("PERM", 96),
+               ("CA", 96), ("CB", 128), ("C1a", 96), ("C2a", 96), ("N1a", 96), ("N2a", 96), ("C1b", 96), ("C2b", 96), ("N1b", 96), ("N2b", 96),
+               ("RMX", 512), ("RMN", 512), ("HOLD", 96), ("MVA", 128), ("MVB", 128), ("MVT", 128), ("SELT", 128), ("Z96", 96), ("P23", 128), ("IHL", 1024),
+               ("D16", 16), ("L16", 16), ("PEN", 128)):
+    _tile("bf", _n, _w)
+for _n, _w in (("MODP", 1), ("WTF", 1), ("COLP", 1), ("COLV", 1), ("C23", 1), ("NM", 8), ("ca", 1), ("cb", 1), ("cc", 1), ("M96", 1), ("THF", 8),
+               ("THC1", 1), ("THC2", 1), ("THC3", 1), ("TH2", 1), ("CNT1", 1), ("CNT2", 1), ("CNT3", 1), ("LIMF", 8), ("T8", 128), ("PW", 96),
+               ("PH", 96), ("WCOL", 8), ("WINV", 8), ("LI96", 96), ("DL", 96), ("WZ", 96), ("WA", 48), ("WB", 24), ("WC", 16), ("DW", 96), ("DMP", 8),
+               ("DMI", 8), ("YPF", 256), ("LO8", 8)):
+    _tile("f", _n, _w)
+for _n, _w in (("PI", 1), ("PJ", 1), ("CN1", 1), ("CN2", 1), ("CN3", 1), ("CM1", 1), ("CM2", 1), ("CM3", 1), ("IH", 512), ("IL", 512)):
+    _tile("i", _n, _w)
+
+SCRATCH = {
+    "bf": ("sbuf", [128, SIZE["bf"]], "bfloat16"), "f": ("sbuf", [128, SIZE["f"]], "float32"),
+    "i": ("sbuf", [128, SIZE["i"]], "int32"), "u": ("sbuf", [128, SIZE["u"]], "uint16"),
+    "clm": ("sbuf", [128, CW], "bfloat16"), "tab": ("sbuf", [128, 4192], "bfloat16"),
+    "who_s": ("sbuf", [128, 192], "int32"), "est_s": ("sbuf", [128, 192], "bfloat16"), "wt_s": ("sbuf", [128, 1], "int32"),
+    "lim_s": ("sbuf", [8, 2], "int32"), "par_s": ("sbuf", [128, 256], "int32"), "ids_s": ("sbuf", [128, 256], "int32"),
+    "yv_s0": ("sbuf", [128, 96], "float32"), "ye_s0": ("sbuf", [128, 96], "bfloat16"),
+    "yv_s1": ("sbuf", [128, 96], "float32"), "ye_s1": ("sbuf", [128, 96], "bfloat16"),
+}
+for _c in range(2):
+    for _t in range(1, 5):
+        SCRATCH["in%d_%d" % (_t, _c)] = ("sbuf", [128, 192], "uint16")
+        SCRATCH["out%d_%d" % (_t, _c)] = ("sbuf", [128, 192], "uint16")
+    for _n in ("pre%d" % _c, "sm%d" % _c, "bg%d_0" % _c, "bg%d_1" % _c):
+        SCRATCH[_n] = ("psum", [128, 512], "float32")
+NLD = 20
+WHO = {"%s%d%d%d" % (_n, _v, _c, _b): "A" for _n in "XP" for _v in range(2) for _c in range(2) for _b in range(3)}
+WHO.update({"F%d%d" % (_c, _b): "A" for _c in range(2) for _b in range(3)})
+WHO.update({_n: "V" for _n in ("X100", "P000", "P001", "P100", "P101")})
+PECY = 0.00042
+SEMAPHORES = ["qV", "qA", "qP", "qG", "snt"] + ["ld%d" % k for k in range(NLD)] + ["arr%d_%d" % (t, c) for t in range(1, 5) for c in range(2)]
+
+
+def route(T, topo, rank, t, ch):
+    n = len(T.cores)
+    src = T.cores[rank]
+    dst = T.cores[(rank + (STEP if t < NV else -STEP * (NV - 1))) % n]
+    if topo.may_write(src, dst):
+        return [src, dst]
+    via = [h for h in topo.cores_of(src) if h != src and topo.die(h) == topo.die(src) and topo.may_write(h, dst)]
+    return [src, via[ch % len(via)], dst]
+
+
+def send(g, T, topo, src, dst, out, in_, arr):
+    rid, pid = topo.addr(dst, src)
+    g.remote_dma(out_ap=out, in_ap=in_, remote_sem=T.sem[arr], local_sem=T.sem["snt"], pid=pid, routing_id=rid, dma_engine_mask=topo.mask(src, dst))
+    return len(topo.engines(src, dst))
+
+
+def helper_program(g, core, T, topo):
+    left = 0
+    for t in range(1, NV + 1):
+        for ch in (1, 0):
+            for r in range(len(T.cores)):
+                way = route(T, topo, r, t, ch)
+                if len(way) == 3 and way[1] == core:
+                    b, a = "in%d_%d" % (t, ch), "arr%d_%d" % (t, ch)
+                    g.wait_ge(T.sem[a], len(topo.engines(way[0], core)))
+                    left += send(g, T, topo, core, way[2], T[b][:], T[b][:], a)
+    if left:
+        g.wait_ge(T.sem["snt"], left)
+
+
+def rank_program(g, core, T, topo):
+    rank = T.rank_of(core)
+    if rank is None:
+        helper_program(g, core, T, topo)
+        return
+    prog = build(g, core, T, topo, rank)
+    emit(g, T, prog, schedule(prog))
+
+
+def schedule(ops):
+    n = len(ops)
+    succ = [[] for _ in range(n)]
+    for k, o in enumerate(ops):
+        for d in o["deps"]:
+            succ[d].append(k)
+    low = [0.0] * n
+    for k in range(n - 1, -1, -1):
+        low[k] = ops[k]["cost"] + ops[k]["lat"] + 0.05 + max([low[s] for s in succ[k]] + [0.0])
+    need = [len(o["deps"]) for o in ops]
+    ready = [0.0] * n
+    avail = {}
+    free = {}
+    for k in range(n):
+        avail.setdefault(ops[k]["q"], [])
+        free[ops[k]["q"]] = 0.0
+        if not need[k]:
+            avail[ops[k]["q"]].append(k)
+    order = {q: [] for q in avail}
+    done = 0
+    while done < n:
+        best = None
+        for q in avail:
+            if not avail[q]:
+                continue
+            t0 = max(free[q], min(ready[k] for k in avail[q]))
+            if best is None or t0 < best[0]:
+                best = (t0, q)
+        t0, q = best
+        cand = [k for k in avail[q] if ready[k] <= t0 + 1e-9]
+        k = max(cand, key=lambda x: (low[x], -x))
+        avail[q].remove(k)
+        order[q].append(k)
+        free[q] = t0 + ops[k]["cost"]
+        end = free[q] + ops[k]["lat"]
+        for s in succ[k]:
+            need[s] -= 1
+            ready[s] = max(ready[s], end + 0.05)
+            if not need[s]:
+                avail[ops[s]["q"]].append(s)
+        done += 1
+    return order
+
+
+def emit(g, T, ops, order):
+    n = len(ops)
+    count = {}
+    tok = [None] * n
+    nld = [0]
+    for q in order:
+        for k in order[q]:
+            o = ops[k]
+            if o["kind"] == "dma":
+                tok[k] = ("ld%d" % nld[0], 16)
+                nld[0] += 1
+            elif o["kind"] == "recv":
+                tok[k] = o["tok"]
+            elif o["kind"] == "send":
+                tok[k] = None
+            else:
+                count[q] = count.get(q, 0) + 1
+                tok[k] = ("q" + q, count[q])
+    pos = {q: 0 for q in order}
+    engine = {"V": g.vector, "A": g.scalar, "P": g.tensor, "G": g, "S": g.sync}
+    seen = {q: {} for q in order}
+    clock = [None] * n
+    left = n
+    while left:
+        moved = False
+        for q in order:
+            while pos[q] < len(order[q]):
+                k = order[q][pos[q]]
+                o = ops[k]
+                if any(clock[d] is None for d in o["deps"]):
+                    break
+                if o["kind"] == "recv":
+                    clock[k] = {tok[k][0]: tok[k][1]}
+                else:
+                    mine = seen[q]
+                    for d in sorted(o["deps"], reverse=True):
+                        if tok[d] is None:
+                            continue
+                        s, v = tok[d]
+                        if mine.get(s, 0) < v:
+                            engine[q].wait_ge(T.sem[s], v)
+                            for s2, v2 in clock[d].items():
+                                if mine.get(s2, 0) < v2:
+                                    mine[s2] = v2
+                    ins = o["fn"]()
+                    if o["kind"] == "dma":
+                        ins.then_inc(T.sem[tok[k][0]], 16)
+                    elif o["kind"] == "op":
+                        ins.then_inc(T.sem[tok[k][0]], 1)
+                    clock[k] = dict(mine)
+                    if tok[k]:
+                        clock[k][tok[k][0]] = tok[k][1]
+                pos[q] += 1
+                left -= 1
+                moved = True
+        if not moved:
+            raise ValueError("order")
+    mine = seen["G"]
+    last = {}
+    for k in range(n):
+        if tok[k] and mine.get(tok[k][0], 0) < tok[k][1]:
+            last[tok[k][0]] = max(last.get(tok[k][0], 0), tok[k][1])
+    for s in last:
+        g.wait_ge(T.sem[s], last[s])
+    g.wait_ge(T.sem["snt"], sum(o["sent"] for o in ops))
+
+
+def build(g, core, T, topo, rank):
+    ops = []
+    wr, rd = {}, {}
+
+    def add(q, fn, r=(), w=(), cost=0.1, lat=0.0, kind="op", tok=None, sent=0):
+        k = len(ops)
+        deps = set()
+        for x in r:
+            deps.update(wr.get(x, []))
+            if x[0] == "#":
+                deps.update(d for d in rd.get(x, []) if ops[d]["q"] != q)
+        for x in w:
+            deps.update(wr.get(x, []))
+            deps.update(rd.get(x, []))
+        for x in r:
+            rd.setdefault(x, []).append(k)
+        for x in w:
+            wr[x] = [k]
+            rd[x] = []
+        deps.discard(k)
+        ops.append({"q": q, "fn": fn, "nm": (tuple(w) + ("",))[0], "deps": sorted(deps), "cost": cost, "lat": lat, "kind": kind, "tok": tok, "sent": sent})
+        return k
+
+    def a(name, lo=0, hi=None, st=1, p=128):
+        kind, off, n = TILES[name]
+        hi = n if hi is None else hi
+        return T[kind][0:p, off + lo:off + hi:st] if st > 1 else T[kind][0:p, off + lo:off + hi]
+
+    def col(name, c=0):
+        return a(name, c, c + 1)
+
+    cyc = 0.00083
+
+    def V(fn, r, w, n):
+        return add("V", fn, r, w, max(64, n) * cyc)
+
+    def S(fn, r, w, n):
+        return add("A", fn, r, w, max(64, n) * cyc)
+
+    def copy(q, out, in_, r, w, cost, scale=None):
+        def fn():
+            if q == "A":
+                return g.scalar.activation(out(), in_(), AF.Copy) if scale is None else g.scalar.activation(out(), in_(), AF.Copy, scale=scale)
+            return g.vector.tensor_copy(out(), in_()) if scale is None else g.vector.tensor_scalar(out(), in_(), scale, None, OP.mult)
+        return add(q, fn, r, w, cost)
+
+    def P(mms, r, w, cycles):
+        def fn():
+            ins = None
+            for m in mms():
+                ins = g.tensor.matmul(*m)
+            return ins
+        return add("P", fn, r, w, cycles * PECY)
+
+    def G(fn, r, w, n):
+        return add("G", fn, r, w, 0.17 + 2 * n * cyc)
+
+    def dma(fn, r, w, q="S", cost=0.1, lat=2.5):
+        return add(q, fn, r, w, cost, lat, kind="dma")
+
+    v, sc = g.vector, g.scalar
+    GATHER = 0.065 + 512 * 1.5 * cyc
+
+    dma(lambda: g.sync.dma_start(T.who_s[:], T.who[:]), (), ("who_s",))
+    dma(lambda: g.sync.dma_start(T.wt_s[:], T.wt[:]), (), ("wt_s",))
+    dma(lambda: g.sync.dma_start(T.est_s[:], T.est[:]), (), ("est_s",))
+    dma(lambda: g.sync.dma_start(T.par_s[:], T.par[:]), (), ("par_s",))
+    dma(lambda: g.sync.dma_start(T.lim_s[:], T.lim[:]), (), ("lim_s",))
+    dma(lambda: g.scalar.dma_start(T.clm[:, 0:4096], T.claim[:]), (), ("clm0",), q="A", lat=6.0)
+    dma(lambda: g.scalar.dma_start(T.clm[:, 4096:8192], T.claim[:]), (), ("clm1",), q="A", lat=9.0)
+    dma(lambda: g.scalar.dma_start(T.clm[:, 8192:CW], T.claim[:, 0:CW - 8192]), (), ("clm2",), q="A", lat=9.0)
+    CLM = ("clm0", "clm1", "clm2")
+
+    def ts(out, in0, s1, s2, o0, o1=None):
+        return v.tensor_scalar(out, in0, s1, s2, o0) if o1 is None else v.tensor_scalar(out, in0, s1, s2, o0, o1)
+
+    G(lambda: g.iota(a("PI"), [[0, 1]], 0, 1), (), ("PI",), 1)
+    V(lambda: ts(a("PJ"), a("PI"), 15, None, OP.bitwise_and), ("PI",), ("PJ",), 1)
+    V(lambda: v.tensor_copy(a("MODP"), a("PJ")), ("PJ",), ("MODP",), 1)
+    for c, (x, s) in enumerate(((0, 16.0), (1, 1.0), (2, 16.0), (3, 1.0))):
+        V(lambda c=c, x=x, s=s: ts(a("NM", c, c + 1), a("MODP"), float(x), s, OP.is_equal, OP.mult), ("MODP",), ("NM%d" % c,), 1)
+    V(lambda: v.tensor_tensor(a("COLP"), a("NM", 0, 1), a("NM", 1, 2), OP.add), ("NM0", "NM1"), ("COLP",), 1)
+    V(lambda: v.tensor_tensor(a("COLV"), a("NM", 2, 3), a("NM", 3, 4), OP.add), ("NM2", "NM3"), ("COLV",), 1)
+    V(lambda: ts(a("C23"), a("COLV"), 0.5, None, OP.is_gt), ("COLV",), ("C23",), 1)
+    V(lambda: v.tensor_copy(a("WTF"), T.wt_s[:]), ("wt_s",), ("WTF",), 1)
+    G(lambda: g.iota(a("TI"), [[-16, 8], [0, 16]], 0, 1, allow_small_or_imprecise_dtypes=True), (), ("TI",), 128)
+    G(lambda: g.iota(a("MVT"), [[0, 8], [1, 16]], 0, 0, allow_small_or_imprecise_dtypes=True), (), ("MVT",), 128)
+    G(lambda: g.affine_select(a("SELT"), a("MVT"), [[-16, 8], [0, 16]], OP.is_ge, -1.0, 0, 1), ("MVT",), ("SELT",), 128)
+    G(lambda: g.affine_select(a("TL"), a("SELT"), [[16, 8], [0, 16]], OP.is_ge, -1.0, 15, -1), ("SELT",), ("TL",), 128)
+    V(lambda: v.memset(a("ONE"), 1.0), (), ("ONE",), 64)
+    G(lambda: g.affine_select(a("I128"), a("ONE"), [[-1, 128]], OP.is_equal, 0.0, 0, 1), ("ONE",), ("I128",), 128)
+    V(lambda: ts(a("BD"), a("TL"), 0.0, None, OP.is_ge), ("TL",), ("BD",), 64)
+    V(lambda: ts(a("WBD"), a("BD"), a("WTF"), None, OP.mult), ("BD", "WTF"), ("WBD",), 64)
+    V(lambda: ts(a("BV"), a("BD"), a("COLV"), None, OP.mult), ("BD", "COLV"), ("BV",), 64)
+    for l in range(16):
+        lo, hi = 128 * l, 128 * l + 128
+        V(lambda l=l, lo=lo, hi=hi: ts(a("SUM", lo, hi), a("TL"), float(l), None, OP.is_equal), ("TL",), ("SUM.%d" % l,), 64)
+        V(lambda l=l, lo=lo, hi=hi: ts(a("WTL", lo, hi), a("TL"), float(l), a("WTF"), OP.is_equal, OP.mult), ("TL", "WTF"), ("WTL.%d" % l,), 64)
+        V(lambda l=l, lo=lo, hi=hi: ts(a("PEX", lo, hi), a("TL"), float(l), a("COLP"), OP.is_equal, OP.mult), ("TL", "COLP"), ("PEX.%d" % l,), 64)
+        V(lambda l=l, lo=lo, hi=hi: ts(a("VEX", lo, hi), a("TL"), float(l), a("COLV"), OP.is_equal, OP.mult), ("TL", "COLV"), ("VEX.%d" % l,), 64)
+        V(lambda l=l, lo=lo, hi=hi: ts(a("EXP", lo, hi), a("TI"), float(l), -256.0, OP.is_equal, OP.mult), ("TI",), ("EXP.%d" % l,), 64)
+    fam = {f: tuple("%s.%d" % (f, l) for l in range(16)) for f in ("SUM", "WTL", "PEX", "VEX", "EXP")}
+    V(lambda: v.memset(a("HALF"), -0.5), (), ("HALF",), 768)
+    sel = lambda out, pat, key, n: G(lambda: g.affine_select(a(out, p=96), a("HALF", 0, n, p=96), pat, OP.is_equal, 0.0, 0, 1), ("HALF",), (key,), n)
+    sel("EM0", [[-1, 96], [0, 16]], "EM0", 1536)
+    sel("PERM", [[-1, 16], [-16, 6]], "PERM", 96)
+    sel("EY0", [[-1, 16], [-16, 6], [0, 16]], "EY0", 1536)
+    sel("EM1", [[-1, 6], [0, 16], [-6, 16]], "EM1", 1536)
+    sel("EY1", [[-16, 6], [0, 16], [-1, 16]], "EY1", 1536)
+    V(lambda: v.memset(a("CA"), 0.4375), (), ("CA",), 64)
+    V(lambda: v.memset(a("CB"), 4.5625), (), ("CB",), 64)
+    V(lambda: v.memset(a("Z96"), 0.0), (), ("Z96",), 64)
+    G(lambda: g.iota(a("C1a"), [[16, 6], [1, 16]], 0, 0, allow_small_or_imprecise_dtypes=True), (), ("C1a",), 96)
+    V(lambda: ts(a("M96"), a("MODP"), 96.0, None, OP.mult), ("MODP",), ("M96",), 1)
+    V(lambda: ts(a("C2a"), a("Z96"), a("M96"), None, OP.add), ("Z96", "M96"), ("C2a",), 64)
+    V(lambda: ts(a("N1a"), a("C1a"), -1.0, -1.0, OP.mult, OP.add), ("C1a",), ("N1a",), 64)
+    V(lambda: ts(a("N2a"), a("C2a"), -1.0, 2048.0, OP.mult, OP.add), ("C2a",), ("N2a",), 64)
+    V(lambda: ts(a("C1b"), a("C1a"), 16.0, None, OP.mult), ("C1a",), ("C1b",), 64)
+    V(lambda: ts(a("C2b"), a("Z96"), a("MODP"), None, OP.add), ("Z96", "MODP"), ("C2b",), 64)
+    V(lambda: ts(a("N1b"), a("C1b"), -1.0, 2048.0, OP.mult, OP.add), ("C1b",), ("N1b",), 64)
+    V(lambda: ts(a("N2b"), a("C2b"), -1.0, -1.0, OP.mult, OP.add), ("C2b",), ("N2b",), 64)
+    V(lambda: ts(a("PEN"), a("I128"), float(2 ** 23), None, OP.mult), ("I128",), ("PEN",), 64)
+    BIG = float(2 ** 30)
+    V(lambda: v.memset(a("RMX"), 0.0), (), ("RMX",), 256)
+    V(lambda: v.memset(a("RMX", 0, 512, 16), -BIG), (), ("RMX",), 64)
+    V(lambda: v.memset(a("RMN"), 0.0), (), ("RMN",), 256)
+    V(lambda: v.memset(a("RMN", 0, 512, 16), BIG), (), ("RMN",), 64)
+    V(lambda: v.memset(a("HOLD"), 1.0), (), ("HOLD",), 64)
+    V(lambda: v.memset(a("HOLD", 0, 96, 16), 0.0), (), ("HOLD",), 64)
+    for s in ("00", "01", "10", "11"):
+        V(lambda s=s: v.memset(a("UH" + s), 0.0), (), ("UH" + s,), 96)
+    G(lambda: g.affine_select(a("P23"), a("ONE"), [[-1, 128]], OP.is_equal, 0.0, -2, 1), ("ONE",), ("P23",), 128)
+    V(lambda: ts(a("MVA"), a("P23"), a("C23"), None, OP.mult), ("P23", "C23"), ("MVA",), 64)
+    V(lambda: ts(a("MVB"), a("I128"), a("C23"), None, OP.mult), ("I128", "C23"), ("MVB",), 64)
+    V(lambda: v.memset(a("PH"), 0.5), (), ("PH",), 96)
+    G(lambda: g.iota(a("LI96"), [[1, 16], [0, 6]], 0, 0, allow_small_or_imprecise_dtypes=True), (), ("LI96",), 96)
+    V(lambda: v.tensor_tensor_scan(a("PW"), a("PH"), a("Z96"), float(2 ** 49), OP.mult, OP.max), ("PH", "Z96"), ("PW",), 96)
+    V(lambda: ts(a("DL"), a("LI96"), a("MODP"), None, OP.is_equal), ("LI96", "MODP"), ("DL",), 96)
+    V(lambda: v.tensor_tensor(a("WZ"), a("DL"), a("PW"), OP.mult), ("DL", "PW"), ("WZ",), 192)
+    for src, dst, n in (("WZ", "WA", 48), ("WA", "WB", 24), ("WB", "WC", 12), ("WC", "WCOL", 6)):
+        V(lambda src=src, dst=dst, n=n: v.tensor_tensor(a(dst, 0, n), a(src, 0, n), a(src, n, 2 * n), OP.add), (src,), (dst,), 96)
+    V(lambda: v.reciprocal(a("WINV", 0, 6), a("WCOL", 0, 6)), ("WCOL",), ("WINV",), 300)
+    G(lambda: g.iota(a("L16"), [[1, 16]], 0, 0, allow_small_or_imprecise_dtypes=True), (), ("L16",), 16)
+    for c in range(6):
+        V(lambda c=c: ts(a("DW", 16 * c, 16 * c + 16), a("L16"), a("MODP"), a("WINV", c, c + 1), OP.is_equal, OP.mult), ("L16", "MODP", "WINV"), ("DW%d" % c,), 16)
+    DW = tuple("DW%d" % c for c in range(6))
+    G(lambda: g.iota(a("DMI", 0, 6), [[16, 6]], 4096, 0, allow_small_or_imprecise_dtypes=True), (), ("DMI",), 6)
+    V(lambda: ts(a("DMP", 0, 6), a("DMI", 0, 6), a("MODP"), None, OP.add), ("DMI", "MODP"), ("DMP",), 6)
+    V(lambda: v.tensor_copy(a("LIMF", 0, 2, p=8), T.lim_s[:]), ("lim_s",), ("LIMF",), 2)
+    V(lambda: v.memset(a("T8", p=8), 1.0), (), ("T8a",), 128)
+    G(lambda: g.affine_select(a("T8", p=8), a("T8", p=8), [[-1, 8], [0, 16]], OP.is_equal, 0.0, 0, 1), ("T8a",), ("T8", "T8a"), 128)
+    P(lambda: [(T.pre1[:, 0:2], a("T8", p=8), a("LIMF", 0, 2, p=8), True, True)], ("T8", "LIMF"), ("#pre1",), 256)
+    V(lambda: v.tensor_copy(a("THF", 0, 2), T.pre1[:, 0:2]), ("#pre1",), ("THF",), 2)
+    V(lambda: ts(a("TH2"), a("THF", 1, 2), 2048.0, None, OP.mult), ("THF",), ("TH2",), 1)
+    G(lambda: g.iota(T.ids_s[:], [[1, 256]], 0, 256), (), ("ids_s",), 256)
+    for h, (src, o) in enumerate(((("par_s"), 0), (("ids_s"), 256))):
+        V(lambda src=src, o=o: ts(a("IH", o, o + 256), T[src][:], 4, 255, OP.logical_shift_right, OP.bitwise_and), (src,), ("IH%d" % h,), 256)
+        V(lambda src=src, o=o: ts(a("IL", o, o + 256), T[src][:], 15, None, OP.bitwise_and), (src,), ("IL%d" % h,), 256)
+        V(lambda o=o: v.tensor_copy(a("IHL", o, o + 256), a("IH", o, o + 256)), ("IH%d" % h,), ("IHLh%d" % h,), 256)
+        V(lambda o=o: v.tensor_copy(a("IHL", 512 + o, 512 + o + 256), a("IL", o, o + 256)), ("IL%d" % h,), ("IHLl%d" % h,), 256)
+    V(lambda: v.memset(T.tab[:], 0.0), (), ("tab",), 2096)
+    for r, (o, key) in enumerate(((0, "IHLh0"), (512, "IHLl0"), (256, "IHLh1"), (768, "IHLl1"))):
+        k = dma(lambda r=r, o=o: g.sync.dma_start(T.tab[r::16, 0:4096], a("IHL", o, o + 256)), (key, "tab"), ("tabr%d" % r,))
+    rows = ["tabr%d" % r for r in range(4)]
+
+    def mod(t, ch):
+        return t % 2
+
+    def pre(t, ch):
+        s = "%d%d" % (t % 2, ch)
+        pb, pk = T["pre%d" % ch], "#pre%d" % ch
+        lo = NC * ch
+        if t == 0:
+            yb, ykey = T.est_s[:, lo:lo + NC], "est_s"
+            vf, vkey = T.who_s[:, lo:lo + NC], "who_s"
+            V(lambda: v.tensor_copy(a("VL" + s), vf), (vkey,), ("VL" + s,), 96)
+            vl, lkey = a("VL" + s), "VL" + s
+            P(lambda: [(pb[:, 0:96], a("WBD"), yb, True, True)], ("WBD", ykey), (pk,), 96)
+            V(lambda: v.tensor_copy(a("UI" + s), pb[:, 0:96]), (pk,), ("UI" + s,), 96)
+            V(lambda: ts(a("UJ" + s), a("UI" + s), 4095, None, OP.bitwise_and), ("UI" + s,), ("UJ" + s,), 96)
+            up, ukey = a("UJ" + s), "UJ" + s
+        else:
+            inb, key = T["in%d_%d" % (t, ch)], "in%d_%d" % (t, ch)
+            V(lambda: v.tensor_copy(a("YB" + s), inb[:, 96:192]), (key,), ("YB" + s,), 96)
+            V(lambda: v.tensor_copy(a("VF" + s), inb[:, 0:96]), (key,), ("VF" + s,), 96)
+            vf, vkey, vl, lkey, yb, ykey = a("VF" + s), "VF" + s, inb[:, 0:96], key, a("YB" + s), "YB" + s
+            P(lambda: [(pb[:, 0:6], a("WTL", 128 * l, 128 * l + 128), a("YB" + s, 6 * l, 6 * l + 6), l == 0, l == 15) for l in range(16)],
+              fam["WTL"] + (ykey,), (pk,), 1024)
+            V(lambda: v.tensor_copy(a("UI" + s, 0, 6), pb[:, 0:6]), (pk,), ("UI" + s,), 6)
+            V(lambda: ts(a("UJ" + s, 0, 6), a("UI" + s, 0, 6), 4095, None, OP.bitwise_and), ("UI" + s,), ("UJ" + s,), 6)
+            V(lambda: v.tensor_copy(a("UH" + s, 0, 96, 16), a("UJ" + s, 0, 6)), ("UJ" + s,), ("UH" + s,), 6)
+            V(lambda: v.tensor_tensor_scan(a("UP" + s), a("HOLD"), a("UH" + s), 0.0, OP.mult, OP.add), ("HOLD", "UH" + s), ("UP" + s,), 96)
+            up, ukey = a("UP" + s), "UP" + s
+        hash_(t, s, "T", vf, vkey, 192, up, ukey, "XL")
+        for b in range(3):
+            copy(WHO["X%d%d%d" % (min(t, 1), ch, b)], lambda b=b: a("X" + s, 512 * b, 512 * b + 512), lambda b=b: T.clm[:].indirect(a("XL" + s, 32 * b, 32 * b + 32)),
+                 ("XL" + s,) + CLM, ("X%s.%d" % (s, b),), GATHER)
+        return vf, vkey, vl, lkey, yb, ykey, up, ukey
+
+    def hash_(t, s, x, vf, vkey, n, up, ukey, out):
+        V(lambda: v.tensor_tensor(a(x + "1" + s), vf, up, OP.mult), (vkey, ukey), (x + "1" + s,), n)
+        V(lambda: ts(a(x + "2" + s), a(x + "1" + s), 5, 4095, OP.logical_shift_right, OP.bitwise_and), (x + "1" + s,), (x + "2" + s,), 96)
+        V(lambda: v.tensor_tensor(a(x + "3" + s), vf, a(x + "2" + s), OP.add), (vkey, x + "2" + s), (x + "3" + s,), n)
+        V(lambda: ts(a(out + s), a(x + "3" + s), 77 * t, None, OP.add), (x + "3" + s,), (out + s,), 96)
+
+    def sl(name, t, l, n0=0, n1=96):
+        if t == 0:
+            return a(name, 96 * l + n0, 96 * l + n1)
+        return a(name, 16 * n0 + l, 16 * (n1 - 1) + l + 1, 16)
+
+    def psum_P(out, f, name, t, r):
+        return [(out, a(f, 128 * l, 128 * l + 128), sl(name, t, l), l == 0, l == 15) for l in range(16)]
+
+    b3 = lambda name: tuple("%s.%d" % (name, b) for b in range(3))
+    state = {}
+
+    def parents(t, ch):
+        s = "%d%d" % (t % 2, ch)
+        vf, vkey, vl, lkey, yb, ykey, up, ukey = state[(t, ch)]
+        pb, pk, sm, sk = T["pre%d" % ch], "#pre%d" % ch, T["sm%d" % ch], "#sm%d" % ch
+        for b in range(3):
+            copy(WHO["P%d%d%d" % (min(t, 1), ch, b)], lambda b=b: a("PR" + s, 512 * b, 512 * b + 512), lambda b=b: T.tab[:, 0:4096].indirect(lst(t, ch, s, b)),
+                 (lkey, "tab") + tuple(rows), ("PR%s.%d" % (s, b),), GATHER)
+        if t == 0:
+            P(lambda: [(pb[:, 0:96], a("PEX", 128 * k, 128 * k + 128), a("PR" + s, k, 1536 - 15 + k, 16), k == 0, k == 15) for k in range(16)],
+              fam["PEX"] + b3("PR" + s), (pk,), 1536)
+            hash_(t, s, "Q", pb[:, 0:96], pk, 96, up, ukey, "ZL")
+            P(lambda: psum_P(sm[:, 0:96], "VEX", "PR" + s, t, 0), fam["VEX"] + b3("PR" + s), (sk,), 1536)
+            V(lambda: v.tensor_copy(a("VF" + s), sm[:, 0:96]), (sk,), ("VF" + s,), 96)
+            P(lambda: psum_P(sm[:, 0:96], "PEX", "PR" + s, t, 0), fam["PEX"] + b3("PR" + s), (sk,), 1536)
+            V(lambda: v.tensor_tensor(a("DV" + s), sm[:, 0:96], a("VF" + s), OP.subtract), (sk, "VF" + s), ("DV" + s,), 96)
+        else:
+            P(lambda: psum_P(sm[:, 0:96], "PEX", "PR" + s, t, 0), fam["PEX"] + b3("PR" + s), (sk,), 1536)
+            hash_(t, s, "Q", sm[:, 0:96], sk, 96, up, ukey, "ZL")
+            V(lambda: v.tensor_tensor(a("DV" + s), sm[:, 0:96], a("VF" + s), OP.subtract), (sk, "VF" + s), ("DV" + s,), 96)
+        for b in range(3):
+            x = (512 * b, 512 * b + 512)
+            add("V", lambda b=b, x=x: v.tensor_tensor(a("D" + s, *x), T.clm[:].indirect(a("ZL" + s, 32 * b, 32 * b + 32)), a("X" + s, *x), OP.subtract),
+                ("ZL" + s, "X%s.%d" % (s, b)) + CLM, ("D%s.%d" % (s, b),), 0.05 + 512 * 1.5 * cyc)
+            S(lambda x=x: sc.activation(a("A" + s, *x), a("D" + s, *x), AF.Abs), ("D%s.%d" % (s, b),), ("A%s.%d" % (s, b),), 512)
+
+    def lst(t, ch, s, b):
+        return a("VL" + s, 32 * b, 32 * b + 32) if t == 0 else T["in%d_%d" % (t, ch)][:, 32 * b:32 * b + 32]
+
+    def dependent(t, ch):
+        s = "%d%d" % (t % 2, ch)
+        sm, sk = T["sm%d" % ch], "#sm%d" % ch
+        th, tkey = (a("THF", 0, 1), "THF") if t == 0 else (a("THC%d" % t), "THC%d" % t)
+        P(lambda: psum_P(sm[:, 0:96], "SUM", "A" + s, t, 0), fam["SUM"] + b3("A" + s), (sk,), 1536)
+        V(lambda: ts(a("DEP" + s), sm[:, 0:96], th, None, OP.is_lt), (sk, tkey), ("DEP" + s,), 96)
+        V(lambda: ts(a("CAN" + s), sm[:, 0:96], th, None, OP.is_ge), (sk, tkey), ("CAN" + s,), 96)
+        for m, out, data0, rkey, op1 in (("DEP", "S1", "RMX", "RMX", OP.max), ("CAN", "S2", "RMN", "RMN", OP.min)):
+            for b in range(3):
+                bank = "bg%d_%d" % (ch, (b + (m == "CAN")) % 2)
+
+                def mms(b=b, m=m, bank=bank):
+                    res = []
+                    for l in range(16):
+                        lo, hi = max(96 * l, 512 * b), min(96 * l + 96, 512 * b + 512)
+                        if lo < hi:
+                            o = T[bank][:, lo - 512 * b:hi - 512 * b]
+                            n0, n1 = lo - 96 * l, hi - 96 * l
+                            res.append((o, a("I128"), sl("X" + s, t, l, n0, n1), True, False))
+                            res.append((o, a("EXP", 128 * l, 128 * l + 128), a(m + s, n0, n1), False, True))
+                    return res
+                P(mms, ("I128", m + s) + fam["EXP"] + b3("X" + s), ("#" + bank,), 1100)
+                V(lambda b=b, out=out, data0=data0, op1=op1, bank=bank: v.tensor_tensor_scan(a(out + s, 512 * b, 512 * b + 512), a(data0), T[bank][:, 0:512], 0.0, OP.add, op1),
+                  ("#" + bank, rkey), ("%s%s.%d" % (out, s, b),), 512)
+        V(lambda: v.tensor_tensor(a("VT" + s), a("DEP" + s), a("DV" + s), OP.mult), ("DEP" + s, "DV" + s), ("VT" + s,), 192)
+        V(lambda: v.tensor_tensor(a("VN" + s), a("VT" + s), a("VF" + s), OP.add), ("VT" + s, "VF" + s), ("VN" + s,), 192)
+        ob, ok = T["out%d_%d" % (t + 1, ch)], "out%d_%d" % (t + 1, ch)
+        if t < NV - 1:
+            V(lambda: v.tensor_copy(ob[:, 0:96], a("VN" + s)), ("VN" + s,), (ok + "v",), 96)
+        else:
+            V(lambda: v.tensor_copy(a("VL" + s), a("VN" + s)), ("VN" + s,), ("VL" + s,), 96)
+            for b in range(3):
+                copy(WHO["F%d%d" % (ch, b)], lambda b=b: a("D" + s, 512 * b, 512 * b + 512), lambda b=b: T.tab[:, 0:4096].indirect(a("VL" + s, 32 * b, 32 * b + 32)),
+                     ("VL" + s, "tab") + tuple(rows), ("D%s.%d" % (s, b),), GATHER)
+            pb, pk = T["pre%d" % ch], "#pre%d" % ch
+            P(lambda: [(pb[:, c:c + 91:6], a("VEX", 128 * k, 128 * k + 128), a("D" + s, 256 * c + 16 * k, 256 * c + 16 * k + 16), k == 0, k == 15)
+                       for c in range(6) for k in range(16)], fam["VEX"] + b3("D" + s), (pk,), 6144)
+            V(lambda: v.tensor_copy(ob[:, 0:96], pb[:, 0:96]), (pk,), (ok + "v",), 96)
+
+    def counter(t):
+        s0, s1 = "%d0" % (t % 2), "%d1" % (t % 2)
+        n = "%d" % (t + 1)
+        P(lambda: [(T.sm0[:, 0:96], a("ONE"), a("DEP" + s0), True, False), (T.sm0[:, 0:96], a("ONE"), a("DEP" + s1), False, True)],
+          ("ONE", "DEP" + s0, "DEP" + s1), ("#sm0",), 192)
+        V(lambda: v.tensor_reduce(a("CNT" + n), T.sm0[:, 0:96], AxisListType.X, OP.add), ("#sm0",), ("CNT" + n,), 96)
+        V(lambda: v.tensor_copy(a("CN" + n), a("CNT" + n)), ("CNT" + n,), ("CN" + n,), 1)
+        V(lambda: ts(a("CM" + n), a("CN" + n), 31, None, OP.bitwise_and), ("CN" + n,), ("CM" + n,), 1)
+        V(lambda: v.tensor_tensor(a("THC" + n), a("CM" + n), a("THF", 0, 1), OP.add), ("CM" + n, "THF"), ("THC" + n,), 1)
+
+    def far(t, s, ch, ext, lhs, lkey):
+        for b in range(3):
+            bank = "bg%d_%d" % (ch, (b + (ext[1] == "Y")) % 2)
+            x = (512 * b, 512 * b + 512)
+            P(lambda b=b, x=x, bank=bank: [(T[bank][:, 0:512], a("I128"), a("X" + s, *x), True, False),
+                                           (T[bank][:, 0:512], a(lhs + s, p=96), a(ext, x[0], x[1], p=96), False, True)],
+              ("I128", "X%s.%d" % (s, b), lkey, ext), ("#" + bank,), 1024)
+            S(lambda x=x, bank=bank: sc.activation(a("A" + s, *x), T[bank][:, 0:512], AF.Abs, scale=2048.0), ("#" + bank,), ("A%s.%d" % (s, b),), 512)
+
+    def truth(t, ch):
+        s = "%d%d" % (t % 2, ch)
+        sm, sk = T["sm%d" % ch], "#sm%d" % ch
+        e = "0" if t == 0 else "1"
+        cs = "a" if t == 0 else "b"
+        vf, vkey, vl, lkey, yb, ykey, up, ukey = state[(t, ch)]
+        P(lambda: [(sm[0:96, 0:128], a("S1" + s, 15, 1536, 16), a("I128"), True, False), (sm[0:96, 0:128], a("S2" + s, 15, 1536, 16), a("I128"), False, False),
+                   (sm[0:96, 0:128], a("CA"), a("CB"), False, True)], b3("S1" + s) + b3("S2" + s) + ("I128", "CA", "CB"), (sk,), 384)
+        V(lambda: ts(a("MT" + s, p=96), sm[0:96, 0:128], float(1.5 * 2 ** 24), float(-1.5 * 2 ** 24), OP.add, OP.add), (sk,), ("MT" + s,), 128)
+        far(t, s, ch, "EM" + e, "MT", "MT" + s)
+        P(lambda: [(sm[:, 0:96], a("PEN"), a("DEP" + s), True, False), (sm[:, 0:96], a("I128"), a("C1" + cs), False, False), (sm[:, 0:96], a("I128"), a("C2" + cs), False, False)] +
+          [(sm[:, 0:96], a("SUM", 128 * l, 128 * l + 128), sl("A" + s, t, l), False, l == 15) for l in range(16)],
+          ("PEN", "DEP" + s, "I128", "C1" + cs, "C2" + cs) + fam["SUM"] + b3("A" + s), (sk,), 1900)
+        V(lambda: v.tensor_tensor_scan(a("M" + s), a("RMN", 0, 96), sm[:, 0:96], 0.0, OP.add, OP.min), (sk, "RMN"), ("M" + s,), 96)
+        V(lambda: v.tensor_copy(a("I1" + s, 0, 6), a("M" + s, 15, 96, 16)), ("M" + s,), ("I1" + s,), 6)
+        V(lambda: ts(a("I2" + s, 0, 6), a("I1" + s, 0, 6), 2047, None, OP.bitwise_and), ("I1" + s,), ("I2" + s,), 6)
+        V(lambda: v.tensor_copy(a("YL" + s, 0, 6), a("I2" + s, 0, 6)), ("I2" + s,), ("YL" + s,), 6)
+        add("V", lambda: v.tensor_copy(a("YG" + s), a("X" + s).indirect(a("YL" + s, 0, 6))), b3("X" + s) + ("YL" + s,), ("YG" + s,), 0.2)
+        P(lambda: [(sm[0:96, 0:128], a("YG" + s), a("I128"), True, True)], ("YG" + s, "I128"), (sk,), 128)
+        S(lambda: sc.activation(a("YT" + s, p=96), sm[0:96, 0:128], AF.Copy, scale=2.0), (sk,), ("YT" + s,), 128)
+        far(t, s, ch, "EY" + e, "YT", "YT" + s)
+        P(lambda: [(sm[:, 0:96], a("YT" + s, p=96), a("PERM", p=96), True, True)], ("YT" + s, "PERM"), (sk,), 96)
+        V(lambda: v.tensor_tensor(a("YS" + s), yb, sm[:, 0:96], OP.subtract), (ykey, sk), ("YS" + s,), 96)
+        V(lambda: ts(a("YH" + s), a("YS" + s), 1, None, OP.logical_shift_right), ("YS" + s,), ("YH" + s,), 96)
+        ob, ok = T["out%d_%d" % (t + 1, ch)], "out%d_%d" % (t + 1, ch)
+        V(lambda: v.tensor_copy(ob[:, 96:192], a("YH" + s)), ("YH" + s,), (ok + "y",), 96)
+        way = route(T, topo, rank, t + 1, ch)
+        b, arr = "in%d_%d" % (t + 1, ch), "arr%d_%d" % (t + 1, ch)
+        n = len(topo.engines(core, way[1]))
+        add("G", lambda: send(g, T, topo, core, way[1], T[b][:], ob[:], arr), (ok + "v", ok + "y"), ("sent%d_%d" % (t, ch),), 0.5, 4.0, kind="send", sent=n)
+        prev = (rank - (STEP if t + 1 < NV else -STEP * (NV - 1))) % len(T.cores)
+        back = route(T, topo, prev, t + 1, ch)
+        add("R%d%d" % (t, ch), None, ("sent%d_%d" % (t, ch),), (b,), 0.0, 0.0, kind="recv", tok=(arr, len(topo.engines(back[-2], core))))
+
+    def asks(t, ch):
+        s = "%d%d" % (t % 2, ch)
+        sm, sk = T["sm%d" % ch], "#sm%d" % ch
+        cs = "a" if t == 0 else "b"
+        P(lambda: [(sm[:, 0:96], a("I128"), a("N1" + cs), True, False), (sm[:, 0:96], a("I128"), a("N2" + cs), False, False)] +
+          [(sm[:, 0:96], a("SUM", 128 * l, 128 * l + 128), sl("A" + s, t, l), False, l == 15) for l in range(16)],
+          ("I128", "N1" + cs, "N2" + cs) + fam["SUM"] + b3("A" + s), (sk,), 1750)
+        V(lambda: v.tensor_tensor_scan(a("MM" + s, 0, 96), a("RMX", 0, 96), sm[:, 0:96], 0.0, OP.add, OP.max), (sk, "RMX"), ("M1" + s,), 96)
+        V(lambda: v.tensor_tensor(a("W" + s, 1, 96), a("MM" + s, 0, 95), sm[:, 1:96], OP.min), (sk, "M1" + s), ("W" + s,), 96)
+        V(lambda: v.tensor_tensor_scan(a("MM" + s, 97, 192), a("RMX", 0, 95), a("W" + s, 1, 96), 0.0, OP.add, OP.max), ("W" + s, "RMX"), ("M2" + s,), 96)
+        V(lambda: v.tensor_copy(a("E1" + s, 0, 12), a("MM" + s, 15, 192, 16)), ("M1" + s, "M2" + s), ("E1" + s,), 12)
+        V(lambda: ts(a("E2" + s, 0, 12), a("E1" + s, 0, 12), 2047, None, OP.bitwise_and), ("E1" + s,), ("E2" + s,), 12)
+        V(lambda: ts(a("AB" + s, 0, 12), a("E2" + s, 0, 12), -1, 2047, OP.mult, OP.add), ("E2" + s,), ("AB" + s,), 12)
+        add("V", lambda: v.tensor_copy(a("G" + s), a("PR" + s).indirect(a("AB" + s, 0, 12))), b3("PR" + s) + ("AB" + s,), ("G" + s,), 0.4)
+        V(lambda: ts(a("ASK" + s, 0, 6), a("MM" + s, 96 + 15, 192, 16), a("TH2"), None, OP.is_ge), ("M2" + s, "TH2"), ("ASK" + s,), 6)
+        V(lambda: v.tensor_tensor(a("AW" + s, 0, 6), a("ASK" + s, 0, 6), a("WCOL", 0, 6), OP.mult), ("ASK" + s, "WCOL"), ("AW" + s,), 12)
+        P(lambda: [(sm[:, 0:96], a("BV"), a("G" + s, 96, 192), True, True)] +
+          [(sm[:, 96:102], a("VEX", 128 * l, 128 * l + 128), a("G" + s, 96 + l, 96 + l + 81, 16), l == 0, l == 15) for l in range(16)] +
+          [(sm[:, 128:224], a("MVA"), a("G" + s, 0, 96), True, False), (sm[:, 128:224], a("MVB"), a("G" + s, 96, 192), False, True)],
+          ("BV", "G" + s, "MVA", "MVB") + fam["VEX"], (sk,), 1400)
+        V(lambda: v.tensor_copy(a("S12" + s, 0, 6), sm[:, 96:102]), (sk,), ("S12" + s,), 6)
+        for c in range(6):
+            V(lambda c=c: ts(a("EE" + s, 96 * c, 96 * c + 96), sm[:, 0:96], a("S12" + s, c, c + 1), a("AW" + s, c, c + 1), OP.is_equal, OP.mult),
+              (sk, "S12" + s, "AW" + s), ("EE%s.%d" % (s, c),), 96)
+        S(lambda: sc.activation(a("DAT" + s), sm[:, 128:224], AF.Copy), (sk,), ("DAT" + s,), 96)
+        P(lambda: [(sm[:, 0:96], a("BD"), a("EE" + s, 96 * c, 96 * c + 96), c == 0, c == 5) for c in range(6)],
+          ("BD",) + tuple("EE%s.%d" % (s, c) for c in range(6)), (sk,), 576)
+        V(lambda: v.tensor_tensor(a("LS" + s, 0, 6), a("S12" + s, 0, 6), a("DMP", 0, 6), OP.subtract), ("S12" + s, "DMP"), ("LS" + s,), 12)
+        V(lambda: v.tensor_tensor(a("TT" + s, 0, 6), a("LS" + s, 0, 6), a("ASK" + s, 0, 6), OP.mult), ("LS" + s, "ASK" + s), ("TT" + s,), 12)
+        V(lambda: v.tensor_tensor(a("R" + s), a("DW"), sm[:, 0:96], OP.mult), DW + (sk,), ("R" + s,), 96)
+        V(lambda: v.tensor_tensor_scan(a("RS" + s), a("HOLD"), a("R" + s), 0.0, OP.mult, OP.max), ("R" + s, "HOLD"), ("RS" + s,), 96)
+        V(lambda: ts(a("WN" + s, 0, 6), a("RS" + s, 15, 96, 16), 2.5, None, OP.is_lt), ("RS" + s,), ("WN" + s,), 6)
+        V(lambda: v.tensor_tensor(a("L2" + s, 0, 6), a("WN" + s, 0, 6), a("TT" + s, 0, 6), OP.mult), ("WN" + s, "TT" + s), ("L2" + s,), 12)
+        V(lambda: v.tensor_tensor(a("RS" + s, 0, 6), a("L2" + s, 0, 6), a("DMP", 0, 6), OP.add), ("L2" + s, "DMP"), ("RS" + s,), 12)
+        V(lambda: v.tensor_copy(a("SL" + s, 0, 6), a("RS" + s, 0, 6)), ("RS" + s,), ("SL" + s,), 6)
+        add("V", lambda: v.tensor_copy(T.tab[:].indirect(a("SL" + s, 0, 6)), a("DAT" + s)), ("SL" + s, "DAT" + s) + tuple(rows), ("tab",), 0.4)
+
+    for ch in (1, 0):
+        state[(0, ch)] = pre(0, ch)
+    for t in range(NV):
+        for stage in (parents, dependent):
+            for ch in (1, 0):
+                stage(t, ch)
+        if t < NV - 1:
+            counter(t)
+        for ch in (1, 0):
+            truth(t, ch)
+        for ch in (1, 0):
+            asks(t, ch)
+        if t < NV - 1:
+            for ch in (1, 0):
+                state[(t + 1, ch)] = pre(t + 1, ch)
+    for ch in (1, 0):
+        b, lo = "in%d_%d" % (NV, ch), NC * ch
+        V(lambda b=b, ch=ch: v.tensor_copy(T["yv_s%d" % ch][:], T[b][:, 0:96]), (b,), ("yvs%d" % ch,), 96)
+        V(lambda b=b, ch=ch: v.tensor_copy(T["ye_s%d" % ch][:], T[b][:, 96:192]), (b,), ("yes%d" % ch,), 96)
+        dma(lambda ch=ch, lo=lo: g.sync.dma_start(T.yv[:, lo:lo + NC], T["yv_s%d" % ch][:]), ("yvs%d" % ch,), ("yv%d" % ch,))
+        dma(lambda ch=ch, lo=lo: g.sync.dma_start(T.ye[:, lo:lo + NC], T["ye_s%d" % ch][:]), ("yes%d" % ch,), ("ye%d" % ch,))
+    P(lambda: [(T.bg0_0[:, 0:256], a("PEX", 128 * c, 128 * c + 128), T.tab[:, 256 * c:256 * c + 256], c == 0, c == 15) for c in range(16)],
+      fam["PEX"] + ("tab",), ("#bg0_0",), 4096)
+    V(lambda: v.tensor_copy(a("YPF"), T.bg0_0[:, 0:256]), ("#bg0_0",), ("YPF",), 256)
+    dma(lambda: g.sync.dma_start(T.yp[:], a("YPF")), ("YPF",), ("yp",))
+    return ops

@@ -25,22 +25,22 @@ for _p in range(2):
                        ("MT", 128), ("YG", 96), ("YT", 128), ("G", 192), ("EE", 576), ("DAT", 96), ("YB", 96)):
             _tile("bf", _n + _s, _w)
         for _n, _w in (("UP", 96), ("VF", 96), ("UH", 96), ("DV", 96), ("VT", 96), ("VN", 96), ("M", 96), ("MM", 192), ("W", 96), ("ASK", 8),
-                       ("AW", 8), ("R", 96), ("RS", 96), ("TT", 8), ("WN", 8), ("LS", 8), ("L2", 8), ("S12", 8)):
+                       ("AW", 8), ("R", 96), ("RS", 96), ("TT", 8), ("WN", 8), ("LS", 8), ("L2", 8), ("S12", 96), ("SD", 96), ("YS", 96)):
             _tile("f", _n + _s, _w)
         for _n, _w in (("UI", 96), ("UJ", 96), ("T1", 96), ("T2", 96), ("T3", 96), ("Q1", 96), ("Q2", 96), ("Q3", 96), ("I1", 8), ("I2", 8),
-                       ("YS", 96), ("YH", 96), ("E1", 16), ("E2", 16)):
+                       ("E1", 16), ("E2", 16)):
             _tile("i", _n + _s, _w)
         for _n, _w in (("XL", 96), ("ZL", 96), ("VL", 96), ("YL", 16), ("AB", 16), ("SL", 16)):
             _tile("u", _n + _s, _w)
 for _n, _w in (("I128", 128), ("TL", 128), ("TI", 128), ("BD", 128), ("WBD", 128), ("BV", 128), ("SUM", 2048), ("WTL", 2048), ("PEX", 2048),
                ("VEX", 2048), ("EXP", 2048), ("ONE", 128), ("HALF", 1536), ("EM0", 1536), ("EM1", 1536), ("EY0", 1536), ("EY1", 1536), ("PERM", 96),
-               ("CA", 96), ("CB", 128), ("C1a", 96), ("C2a", 96), ("N1a", 96), ("N2a", 96), ("C1b", 96), ("C2b", 96), ("N1b", 96), ("N2b", 96),
+               ("CA", 96), ("CB", 128), ("H96", 96), ("C1a", 96), ("C2a", 96), ("N1a", 96), ("N2a", 96), ("C1b", 96), ("C2b", 96), ("N1b", 96), ("N2b", 96),
                ("RMX", 512), ("RMN", 512), ("HOLD", 96), ("MVA", 128), ("MVB", 128), ("MVT", 128), ("SELT", 128), ("Z96", 96), ("P23", 128), ("IHL", 1024),
                ("D16", 16), ("L16", 16), ("PEN", 128)):
     _tile("bf", _n, _w)
 for _n, _w in (("MODP", 1), ("WTF", 1), ("COLP", 1), ("COLV", 1), ("C23", 1), ("NM", 8), ("ca", 1), ("cb", 1), ("cc", 1), ("M96", 1), ("THF", 8),
                ("THC1", 1), ("THC2", 1), ("THC3", 1), ("TH2", 1), ("CNT1", 1), ("CNT2", 1), ("CNT3", 1), ("LIMF", 8), ("T8", 128), ("PW", 96),
-               ("PH", 96), ("WCOL", 8), ("WINV", 8), ("LI96", 96), ("DL", 96), ("WZ", 96), ("WA", 48), ("WB", 24), ("WC", 16), ("DW", 96), ("DMP", 8),
+               ("PH", 96), ("WCOL", 8), ("WINV", 8), ("LI96", 96), ("DL", 96), ("WZ", 96), ("WA", 48), ("WB", 24), ("WC", 16), ("DW", 96), ("D96", 96), ("DMP", 8),
                ("DMI", 8), ("YPF", 256), ("LO8", 8)):
     _tile("f", _n, _w)
 for _n, _w in (("PI", 1), ("PJ", 1), ("CN1", 1), ("CN2", 1), ("CN3", 1), ("CM1", 1), ("CM2", 1), ("CM3", 1), ("IH", 512), ("IL", 512)):
@@ -57,16 +57,21 @@ SCRATCH = {
 }
 for _c in range(2):
     for _t in range(1, 5):
-        SCRATCH["in%d_%d" % (_t, _c)] = ("sbuf", [128, 192], "uint16")
-        SCRATCH["out%d_%d" % (_t, _c)] = ("sbuf", [128, 192], "uint16")
+        for _n in ("inv", "iny", "outv", "outy"):
+            SCRATCH["%s%d_%d" % (_n, _t, _c)] = ("sbuf", [128, 96], "uint16")
     for _n in ("pre%d" % _c, "sm%d" % _c, "bg%d_0" % _c, "bg%d_1" % _c):
         SCRATCH[_n] = ("psum", [128, 512], "float32")
 NLD = 20
 WHO = {"%s%d%d%d" % (_n, _v, _c, _b): "A" for _n in "XP" for _v in range(2) for _c in range(2) for _b in range(3)}
 WHO.update({"F%d%d" % (_c, _b): "A" for _c in range(2) for _b in range(3)})
-WHO.update({_n: "V" for _n in ("X100", "P000", "P001", "P100", "P101")})
+WHO.update({_n: "V" for _n in ("F01", "F02", "F10", "F12", "P000", "P001", "P002", "P010", "P110", "P112")})
 PECY = 0.00042
-SEMAPHORES = ["qV", "qA", "qP", "qG", "snt"] + ["ld%d" % k for k in range(NLD)] + ["arr%d_%d" % (t, c) for t in range(1, 5) for c in range(2)]
+SCOPY = (("S1", 0), ("S2", 0))
+FARV = (("M", 0),)
+HOP = 0.1
+FIXV, FIXA = 0.02, 0.02
+LEAD = 2.0
+SEMAPHORES = ["qV", "qA", "qP", "qG", "snt"] + ["ld%d" % k for k in range(NLD)] + ["arr%s%d_%d" % (x, t, c) for x in "vy" for t in range(1, 5) for c in range(2)]
 
 
 def route(T, topo, rank, t, ch):
@@ -86,15 +91,16 @@ def send(g, T, topo, src, dst, out, in_, arr):
 
 
 def helper_program(g, core, T, topo):
-    left = 0
+    left, legs = 0, []
     for t in range(1, NV + 1):
         for ch in (1, 0):
             for r in range(len(T.cores)):
                 way = route(T, topo, r, t, ch)
                 if len(way) == 3 and way[1] == core:
-                    b, a = "in%d_%d" % (t, ch), "arr%d_%d" % (t, ch)
-                    g.wait_ge(T.sem[a], len(topo.engines(way[0], core)))
-                    left += send(g, T, topo, core, way[2], T[b][:], T[b][:], a)
+                    legs += [(t, x == "y", 1 - ch, "in%s%d_%d" % (x, t, ch), "arr%s%d_%d" % (x, t, ch), way) for x in "vy"]
+    for _, _, _, b, a, way in sorted(legs):
+        g.wait_ge(T.sem[a], len(topo.engines(way[0], core)))
+        left += send(g, T, topo, core, way[2], T[b][:], T[b][:], a)
     if left:
         g.wait_ge(T.sem["snt"], left)
 
@@ -116,7 +122,9 @@ def schedule(ops):
             succ[d].append(k)
     low = [0.0] * n
     for k in range(n - 1, -1, -1):
-        low[k] = ops[k]["cost"] + ops[k]["lat"] + 0.05 + max([low[s] for s in succ[k]] + [0.0])
+        low[k] = ops[k]["cost"] + ops[k]["lat"] + HOP + max([low[s] for s in succ[k]] + [0.0])
+    for k in range(n):
+        low[k] += LEAD * ops[k]["ch"] + ops[k]["pri"]
     need = [len(o["deps"]) for o in ops]
     ready = [0.0] * n
     avail = {}
@@ -145,7 +153,7 @@ def schedule(ops):
         end = free[q] + ops[k]["lat"]
         for s in succ[k]:
             need[s] -= 1
-            ready[s] = max(ready[s], end + 0.05)
+            ready[s] = max(ready[s], end + HOP)
             if not need[s]:
                 avail[ops[s]["q"]].append(s)
         done += 1
@@ -222,6 +230,7 @@ def emit(g, T, ops, order):
 def build(g, core, T, topo, rank):
     ops = []
     wr, rd = {}, {}
+    now = [0]
 
     def add(q, fn, r=(), w=(), cost=0.1, lat=0.0, kind="op", tok=None, sent=0):
         k = len(ops)
@@ -239,7 +248,7 @@ def build(g, core, T, topo, rank):
             wr[x] = [k]
             rd[x] = []
         deps.discard(k)
-        ops.append({"q": q, "fn": fn, "nm": (tuple(w) + ("",))[0], "deps": sorted(deps), "cost": cost, "lat": lat, "kind": kind, "tok": tok, "sent": sent})
+        ops.append({"q": q, "fn": fn, "nm": (tuple(w) + ("",))[0], "deps": sorted(deps), "ch": now[0], "pri": 0.0, "cost": cost, "lat": lat, "kind": kind, "tok": tok, "sent": sent})
         return k
 
     def a(name, lo=0, hi=None, st=1, p=128):
@@ -253,10 +262,10 @@ def build(g, core, T, topo, rank):
     cyc = 0.00083
 
     def V(fn, r, w, n):
-        return add("V", fn, r, w, max(64, n) * cyc)
+        return add("V", fn, r, w, FIXV + max(64, n) * cyc)
 
     def S(fn, r, w, n):
-        return add("A", fn, r, w, max(64, n) * cyc)
+        return add("A", fn, r, w, FIXA + max(64, n) * cyc)
 
     def copy(q, out, in_, r, w, cost, scale=None):
         def fn():
@@ -316,11 +325,13 @@ def build(g, core, T, topo, rank):
     for l in range(16):
         lo, hi = 128 * l, 128 * l + 128
         V(lambda l=l, lo=lo, hi=hi: ts(a("SUM", lo, hi), a("TL"), float(l), None, OP.is_equal), ("TL",), ("SUM.%d" % l,), 64)
-        V(lambda l=l, lo=lo, hi=hi: ts(a("WTL", lo, hi), a("TL"), float(l), a("WTF"), OP.is_equal, OP.mult), ("TL", "WTF"), ("WTL.%d" % l,), 64)
-        V(lambda l=l, lo=lo, hi=hi: ts(a("PEX", lo, hi), a("TL"), float(l), a("COLP"), OP.is_equal, OP.mult), ("TL", "COLP"), ("PEX.%d" % l,), 64)
-        V(lambda l=l, lo=lo, hi=hi: ts(a("VEX", lo, hi), a("TL"), float(l), a("COLV"), OP.is_equal, OP.mult), ("TL", "COLV"), ("VEX.%d" % l,), 64)
         V(lambda l=l, lo=lo, hi=hi: ts(a("EXP", lo, hi), a("TI"), float(l), -256.0, OP.is_equal, OP.mult), ("TI",), ("EXP.%d" % l,), 64)
-    fam = {f: tuple("%s.%d" % (f, l) for l in range(16)) for f in ("SUM", "WTL", "PEX", "VEX", "EXP")}
+    fam = {f: tuple("%s.%d" % (f, l) for l in range(16)) for f in ("SUM", "EXP")}
+    fam.update({f: tuple("%s.%d" % (f, h) for h in range(2)) for f in ("WTL", "PEX", "VEX")})
+    for f, c in (("PEX", "COLP"), ("VEX", "COLV"), ("WTL", "WTF")):
+        for h in range(2):
+            S(lambda f=f, c=c, h=h: sc.activation(a(f, 1024 * h, 1024 * h + 1024), a("SUM", 1024 * h, 1024 * h + 1024), AF.Copy, scale=a(c)),
+              (c,) + fam["SUM"][8 * h:8 * h + 8], ("%s.%d" % (f, h),), 1024)
     V(lambda: v.memset(a("HALF"), -0.5), (), ("HALF",), 768)
     sel = lambda out, pat, key, n: G(lambda: g.affine_select(a(out, p=96), a("HALF", 0, n, p=96), pat, OP.is_equal, 0.0, 0, 1), ("HALF",), (key,), n)
     sel("EM0", [[-1, 96], [0, 16]], "EM0", 1536)
@@ -330,7 +341,9 @@ def build(g, core, T, topo, rank):
     sel("EY1", [[-16, 6], [0, 16], [-1, 16]], "EY1", 1536)
     V(lambda: v.memset(a("CA"), 0.4375), (), ("CA",), 64)
     V(lambda: v.memset(a("CB"), 4.5625), (), ("CB",), 64)
-    V(lambda: v.memset(a("Z96"), 0.0), (), ("Z96",), 64)
+    flat = lambda out, n, x=0: G(lambda: g.iota(a(out), [[0, n]], x, 0, allow_small_or_imprecise_dtypes=True), (), (out,), n)
+    V(lambda: v.memset(a("H96"), 0.5), (), ("H96",), 64)
+    flat("Z96", 96)
     G(lambda: g.iota(a("C1a"), [[16, 6], [1, 16]], 0, 0, allow_small_or_imprecise_dtypes=True), (), ("C1a",), 96)
     V(lambda: ts(a("M96"), a("MODP"), 96.0, None, OP.mult), ("MODP",), ("M96",), 1)
     V(lambda: ts(a("C2a"), a("Z96"), a("M96"), None, OP.add), ("Z96", "M96"), ("C2a",), 64)
@@ -342,14 +355,13 @@ def build(g, core, T, topo, rank):
     V(lambda: ts(a("N2b"), a("C2b"), -1.0, -1.0, OP.mult, OP.add), ("C2b",), ("N2b",), 64)
     V(lambda: ts(a("PEN"), a("I128"), float(2 ** 23), None, OP.mult), ("I128",), ("PEN",), 64)
     BIG = float(2 ** 30)
-    V(lambda: v.memset(a("RMX"), 0.0), (), ("RMX",), 256)
-    V(lambda: v.memset(a("RMX", 0, 512, 16), -BIG), (), ("RMX",), 64)
-    V(lambda: v.memset(a("RMN"), 0.0), (), ("RMN",), 256)
-    V(lambda: v.memset(a("RMN", 0, 512, 16), BIG), (), ("RMN",), 64)
-    V(lambda: v.memset(a("HOLD"), 1.0), (), ("HOLD",), 64)
-    V(lambda: v.memset(a("HOLD", 0, 96, 16), 0.0), (), ("HOLD",), 64)
+    flat("RMX", 512)
+    G(lambda: g.affine_select(a("RMX"), a("RMX"), [[0, 32], [1, 16]], OP.not_equal, -BIG, 0, 0), ("RMX",), ("RMX",), 512)
+    S(lambda: sc.activation(a("RMN"), a("RMX"), AF.Copy, scale=-1.0), ("RMX",), ("RMN",), 512)
+    flat("HOLD", 96, 1)
+    G(lambda: g.affine_select(a("HOLD"), a("HOLD"), [[0, 6], [1, 16]], OP.not_equal, 0.0, 0, 0), ("HOLD",), ("HOLD",), 96)
     for s in ("00", "01", "10", "11"):
-        V(lambda s=s: v.memset(a("UH" + s), 0.0), (), ("UH" + s,), 96)
+        flat("UH" + s, 96)
     G(lambda: g.affine_select(a("P23"), a("ONE"), [[-1, 128]], OP.is_equal, 0.0, -2, 1), ("ONE",), ("P23",), 128)
     V(lambda: ts(a("MVA"), a("P23"), a("C23"), None, OP.mult), ("P23", "C23"), ("MVA",), 64)
     V(lambda: ts(a("MVB"), a("I128"), a("C23"), None, OP.mult), ("I128", "C23"), ("MVB",), 64)
@@ -364,7 +376,9 @@ def build(g, core, T, topo, rank):
     G(lambda: g.iota(a("L16"), [[1, 16]], 0, 0, allow_small_or_imprecise_dtypes=True), (), ("L16",), 16)
     for c in range(6):
         V(lambda c=c: ts(a("DW", 16 * c, 16 * c + 16), a("L16"), a("MODP"), a("WINV", c, c + 1), OP.is_equal, OP.mult), ("L16", "MODP", "WINV"), ("DW%d" % c,), 16)
+        V(lambda c=c: ts(a("D96", 16 * c, 16 * c + 16), a("L16"), a("MODP"), None, OP.is_equal), ("L16", "MODP"), ("D96.%d" % c,), 16)
     DW = tuple("DW%d" % c for c in range(6))
+    D96 = tuple("D96.%d" % c for c in range(6))
     G(lambda: g.iota(a("DMI", 0, 6), [[16, 6]], 4096, 0, allow_small_or_imprecise_dtypes=True), (), ("DMI",), 6)
     V(lambda: ts(a("DMP", 0, 6), a("DMI", 0, 6), a("MODP"), None, OP.add), ("DMI", "MODP"), ("DMP",), 6)
     V(lambda: v.tensor_copy(a("LIMF", 0, 2, p=8), T.lim_s[:]), ("lim_s",), ("LIMF",), 2)
@@ -401,10 +415,10 @@ def build(g, core, T, topo, rank):
             V(lambda: ts(a("UJ" + s), a("UI" + s), 4095, None, OP.bitwise_and), ("UI" + s,), ("UJ" + s,), 96)
             up, ukey = a("UJ" + s), "UJ" + s
         else:
-            inb, key = T["in%d_%d" % (t, ch)], "in%d_%d" % (t, ch)
-            V(lambda: v.tensor_copy(a("YB" + s), inb[:, 96:192]), (key,), ("YB" + s,), 96)
-            V(lambda: v.tensor_copy(a("VF" + s), inb[:, 0:96]), (key,), ("VF" + s,), 96)
-            vf, vkey, vl, lkey, yb, ykey = a("VF" + s), "VF" + s, inb[:, 0:96], key, a("YB" + s), "YB" + s
+            inv, iny, key, key2 = T["inv%d_%d" % (t, ch)], T["iny%d_%d" % (t, ch)], "inv%d_%d" % (t, ch), "iny%d_%d" % (t, ch)
+            V(lambda: ts(a("YB" + s), iny[:], 0.5, None, OP.mult), (key2,), ("YB" + s,), 48)
+            V(lambda: v.tensor_copy(a("VF" + s), inv[:]), (key,), ("VF" + s,), 96)
+            vf, vkey, vl, lkey, yb, ykey = a("VF" + s), "VF" + s, inv[:], key, a("YB" + s), "YB" + s
             P(lambda: [(pb[:, 0:6], a("WTL", 128 * l, 128 * l + 128), a("YB" + s, 6 * l, 6 * l + 6), l == 0, l == 15) for l in range(16)],
               fam["WTL"] + (ykey,), (pk,), 1024)
             V(lambda: v.tensor_copy(a("UI" + s, 0, 6), pb[:, 0:6]), (pk,), ("UI" + s,), 6)
@@ -461,7 +475,7 @@ def build(g, core, T, topo, rank):
             S(lambda x=x: sc.activation(a("A" + s, *x), a("D" + s, *x), AF.Abs), ("D%s.%d" % (s, b),), ("A%s.%d" % (s, b),), 512)
 
     def lst(t, ch, s, b):
-        return a("VL" + s, 32 * b, 32 * b + 32) if t == 0 else T["in%d_%d" % (t, ch)][:, 32 * b:32 * b + 32]
+        return a("VL" + s, 32 * b, 32 * b + 32) if t == 0 else T["inv%d_%d" % (t, ch)][:, 32 * b:32 * b + 32]
 
     def dependent(t, ch):
         s = "%d%d" % (t % 2, ch)
@@ -469,7 +483,7 @@ def build(g, core, T, topo, rank):
         th, tkey = (a("THF", 0, 1), "THF") if t == 0 else (a("THC%d" % t), "THC%d" % t)
         P(lambda: psum_P(sm[:, 0:96], "SUM", "A" + s, t, 0), fam["SUM"] + b3("A" + s), (sk,), 1536)
         V(lambda: ts(a("DEP" + s), sm[:, 0:96], th, None, OP.is_lt), (sk, tkey), ("DEP" + s,), 96)
-        V(lambda: ts(a("CAN" + s), sm[:, 0:96], th, None, OP.is_ge), (sk, tkey), ("CAN" + s,), 96)
+        S(lambda: sc.activation(a("CAN" + s), a("DEP" + s), AF.Copy, bias=1.0, scale=-1.0), ("DEP" + s,), ("CAN" + s,), 96)
         for m, out, data0, rkey, op1 in (("DEP", "S1", "RMX", "RMX", OP.max), ("CAN", "S2", "RMN", "RMN", OP.min)):
             for b in range(3):
                 bank = "bg%d_%d" % (ch, (b + (m == "CAN")) % 2)
@@ -485,22 +499,31 @@ def build(g, core, T, topo, rank):
                             res.append((o, a("EXP", 128 * l, 128 * l + 128), a(m + s, n0, n1), False, True))
                     return res
                 P(mms, ("I128", m + s) + fam["EXP"] + b3("X" + s), ("#" + bank,), 1100)
+                if (out, b) in SCOPY:
+                    S(lambda b=b, bank=bank: sc.activation(a("D" + s, 512 * b, 512 * b + 512), T[bank][:, 0:512], AF.Copy), ("#" + bank,), ("D%s.%d" % (s, b),), 512)
+                    V(lambda b=b, out=out, data0=data0, op1=op1: v.tensor_tensor_scan(a(out + s, 512 * b, 512 * b + 512), a(data0), a("D" + s, 512 * b, 512 * b + 512), 0.0, OP.add, op1),
+                      ("D%s.%d" % (s, b), rkey), ("%s%s.%d" % (out, s, b),), 256)
+                    continue
                 V(lambda b=b, out=out, data0=data0, op1=op1, bank=bank: v.tensor_tensor_scan(a(out + s, 512 * b, 512 * b + 512), a(data0), T[bank][:, 0:512], 0.0, OP.add, op1),
                   ("#" + bank, rkey), ("%s%s.%d" % (out, s, b),), 512)
         V(lambda: v.tensor_tensor(a("VT" + s), a("DEP" + s), a("DV" + s), OP.mult), ("DEP" + s, "DV" + s), ("VT" + s,), 192)
         V(lambda: v.tensor_tensor(a("VN" + s), a("VT" + s), a("VF" + s), OP.add), ("VT" + s, "VF" + s), ("VN" + s,), 192)
-        ob, ok = T["out%d_%d" % (t + 1, ch)], "out%d_%d" % (t + 1, ch)
+        ob, ok = T["outv%d_%d" % (t + 1, ch)], "outv%d_%d" % (t + 1, ch)
         if t < NV - 1:
-            V(lambda: v.tensor_copy(ob[:, 0:96], a("VN" + s)), ("VN" + s,), (ok + "v",), 96)
+            V(lambda: v.tensor_copy(ob[:], a("VN" + s)), ("VN" + s,), (ok,), 96)
         else:
             V(lambda: v.tensor_copy(a("VL" + s), a("VN" + s)), ("VN" + s,), ("VL" + s,), 96)
             for b in range(3):
                 copy(WHO["F%d%d" % (ch, b)], lambda b=b: a("D" + s, 512 * b, 512 * b + 512), lambda b=b: T.tab[:, 0:4096].indirect(a("VL" + s, 32 * b, 32 * b + 32)),
                      ("VL" + s, "tab") + tuple(rows), ("D%s.%d" % (s, b),), GATHER)
             pb, pk = T["pre%d" % ch], "#pre%d" % ch
-            P(lambda: [(pb[:, c:c + 91:6], a("VEX", 128 * k, 128 * k + 128), a("D" + s, 256 * c + 16 * k, 256 * c + 16 * k + 16), k == 0, k == 15)
-                       for c in range(6) for k in range(16)], fam["VEX"] + b3("D" + s), (pk,), 6144)
-            V(lambda: v.tensor_copy(ob[:, 0:96], pb[:, 0:96]), (pk,), (ok + "v",), 96)
+            for c in range(6):
+                P(lambda c=c: [(pb[:, c:c + 91:6], a("VEX", 128 * k, 128 * k + 128), a("D" + s, 256 * c + 16 * k, 256 * c + 16 * k + 16), k == 0, k == 15)
+                               for k in range(16)], fam["VEX"] + ("D%s.%d" % (s, c // 2),), (pk,), 1024)
+            V(lambda: v.tensor_copy(ob[:], pb[:, 0:96]), (pk,), (ok,), 96)
+
+    def names_leave(t, ch):
+        leave("v", t, ch)
 
     def counter(t):
         s0, s1 = "%d0" % (t % 2), "%d1" % (t % 2)
@@ -516,6 +539,11 @@ def build(g, core, T, topo, rank):
         for b in range(3):
             bank = "bg%d_%d" % (ch, (b + (ext[1] == "Y")) % 2)
             x = (512 * b, 512 * b + 512)
+            if (ext[1], b) in FARV:
+                P(lambda b=b, x=x, bank=bank: [(T[bank][:, 0:512], a(lhs + s, p=96), a(ext, x[0], x[1], p=96), True, True)], (lkey, ext), ("#" + bank,), 512)
+                V(lambda x=x, bank=bank: v.tensor_tensor(a("D" + s, *x), a("X" + s, *x), T[bank][:, 0:512], OP.add), ("#" + bank, "X%s.%d" % (s, b)), ("D%s.%d" % (s, b),), 512)
+                S(lambda x=x: sc.activation(a("A" + s, *x), a("D" + s, *x), AF.Abs, scale=2048.0), ("D%s.%d" % (s, b),), ("A%s.%d" % (s, b),), 512)
+                continue
             P(lambda b=b, x=x, bank=bank: [(T[bank][:, 0:512], a("I128"), a("X" + s, *x), True, False),
                                            (T[bank][:, 0:512], a(lhs + s, p=96), a(ext, x[0], x[1], p=96), False, True)],
               ("I128", "X%s.%d" % (s, b), lkey, ext), ("#" + bank,), 1024)
@@ -531,9 +559,10 @@ def build(g, core, T, topo, rank):
                    (sm[0:96, 0:128], a("CA"), a("CB"), False, True)], b3("S1" + s) + b3("S2" + s) + ("I128", "CA", "CB"), (sk,), 384)
         V(lambda: ts(a("MT" + s, p=96), sm[0:96, 0:128], float(1.5 * 2 ** 24), float(-1.5 * 2 ** 24), OP.add, OP.add), (sk,), ("MT" + s,), 128)
         far(t, s, ch, "EM" + e, "MT", "MT" + s)
-        P(lambda: [(sm[:, 0:96], a("PEN"), a("DEP" + s), True, False), (sm[:, 0:96], a("I128"), a("C1" + cs), False, False), (sm[:, 0:96], a("I128"), a("C2" + cs), False, False)] +
-          [(sm[:, 0:96], a("SUM", 128 * l, 128 * l + 128), sl("A" + s, t, l), False, l == 15) for l in range(16)],
-          ("PEN", "DEP" + s, "I128", "C1" + cs, "C2" + cs) + fam["SUM"] + b3("A" + s), (sk,), 1900)
+        P(lambda: [(sm[:, 0:96], a("PEN"), a("DEP" + s), True, False), (sm[:, 0:96], a("I128"), a("C1" + cs), False, False), (sm[:, 0:96], a("I128"), a("C2" + cs), False, False)],
+          ("PEN", "DEP" + s, "I128", "C1" + cs, "C2" + cs), (sk,), 288)
+        P(lambda: [(sm[:, 0:96], a("SUM", 128 * l, 128 * l + 128), sl("A" + s, t, l), False, l == 15) for l in range(16)],
+          fam["SUM"] + b3("A" + s), (sk,), 1536)
         V(lambda: v.tensor_tensor_scan(a("M" + s), a("RMN", 0, 96), sm[:, 0:96], 0.0, OP.add, OP.min), (sk, "RMN"), ("M" + s,), 96)
         V(lambda: v.tensor_copy(a("I1" + s, 0, 6), a("M" + s, 15, 96, 16)), ("M" + s,), ("I1" + s,), 6)
         V(lambda: ts(a("I2" + s, 0, 6), a("I1" + s, 0, 6), 2047, None, OP.bitwise_and), ("I1" + s,), ("I2" + s,), 6)
@@ -542,26 +571,31 @@ def build(g, core, T, topo, rank):
         P(lambda: [(sm[0:96, 0:128], a("YG" + s), a("I128"), True, True)], ("YG" + s, "I128"), (sk,), 128)
         S(lambda: sc.activation(a("YT" + s, p=96), sm[0:96, 0:128], AF.Copy, scale=2.0), (sk,), ("YT" + s,), 128)
         far(t, s, ch, "EY" + e, "YT", "YT" + s)
-        P(lambda: [(sm[:, 0:96], a("YT" + s, p=96), a("PERM", p=96), True, True)], ("YT" + s, "PERM"), (sk,), 96)
+        P(lambda: [(sm[:, 0:96], a("YT" + s, p=96), a("PERM", p=96), True, False), (sm[:, 0:96], a("I128"), a("H96"), False, True)],
+          ("YT" + s, "PERM", "I128", "H96"), (sk,), 192)
         V(lambda: v.tensor_tensor(a("YS" + s), yb, sm[:, 0:96], OP.subtract), (ykey, sk), ("YS" + s,), 96)
-        V(lambda: ts(a("YH" + s), a("YS" + s), 1, None, OP.logical_shift_right), ("YS" + s,), ("YH" + s,), 96)
-        ob, ok = T["out%d_%d" % (t + 1, ch)], "out%d_%d" % (t + 1, ch)
-        V(lambda: v.tensor_copy(ob[:, 96:192], a("YH" + s)), ("YH" + s,), (ok + "y",), 96)
+        ob, ok = T["outy%d_%d" % (t + 1, ch)], "outy%d_%d" % (t + 1, ch)
+        V(lambda: ts(ob[:], a("YS" + s), float(1.5 * 2 ** 24), float(-1.5 * 2 ** 24), OP.add, OP.add), ("YS" + s,), (ok,), 96)
+        leave("y", t, ch)
+
+    def leave(x, t, ch):
+        ob, ok = T["out%s%d_%d" % (x, t + 1, ch)], "out%s%d_%d" % (x, t + 1, ch)
         way = route(T, topo, rank, t + 1, ch)
-        b, arr = "in%d_%d" % (t + 1, ch), "arr%d_%d" % (t + 1, ch)
+        b, arr = "in%s%d_%d" % (x, t + 1, ch), "arr%s%d_%d" % (x, t + 1, ch)
         n = len(topo.engines(core, way[1]))
-        add("G", lambda: send(g, T, topo, core, way[1], T[b][:], ob[:], arr), (ok + "v", ok + "y"), ("sent%d_%d" % (t, ch),), 0.5, 4.0, kind="send", sent=n)
+        add("G", lambda: send(g, T, topo, core, way[1], T[b][:], ob[:], arr), (ok,), ("sent%s%d_%d" % (x, t, ch),), 0.5, 6.0, kind="send", sent=n)
         prev = (rank - (STEP if t + 1 < NV else -STEP * (NV - 1))) % len(T.cores)
         back = route(T, topo, prev, t + 1, ch)
-        add("R%d%d" % (t, ch), None, ("sent%d_%d" % (t, ch),), (b,), 0.0, 0.0, kind="recv", tok=(arr, len(topo.engines(back[-2], core))))
+        add("R%s%d%d" % (x, t, ch), None, ("sent%s%d_%d" % (x, t, ch),), (b,), 0.0, 0.0, kind="recv", tok=(arr, len(topo.engines(back[-2], core))))
 
     def asks(t, ch):
         s = "%d%d" % (t % 2, ch)
         sm, sk = T["sm%d" % ch], "#sm%d" % ch
         cs = "a" if t == 0 else "b"
-        P(lambda: [(sm[:, 0:96], a("I128"), a("N1" + cs), True, False), (sm[:, 0:96], a("I128"), a("N2" + cs), False, False)] +
-          [(sm[:, 0:96], a("SUM", 128 * l, 128 * l + 128), sl("A" + s, t, l), False, l == 15) for l in range(16)],
-          ("I128", "N1" + cs, "N2" + cs) + fam["SUM"] + b3("A" + s), (sk,), 1750)
+        P(lambda: [(sm[:, 0:96], a("I128"), a("N1" + cs), True, False), (sm[:, 0:96], a("I128"), a("N2" + cs), False, False)],
+          ("I128", "N1" + cs, "N2" + cs), (sk,), 192)
+        P(lambda: [(sm[:, 0:96], a("SUM", 128 * l, 128 * l + 128), sl("A" + s, t, l), False, l == 15) for l in range(16)],
+          fam["SUM"] + b3("A" + s), (sk,), 1536)
         V(lambda: v.tensor_tensor_scan(a("MM" + s, 0, 96), a("RMX", 0, 96), sm[:, 0:96], 0.0, OP.add, OP.max), (sk, "RMX"), ("M1" + s,), 96)
         V(lambda: v.tensor_tensor(a("W" + s, 1, 96), a("MM" + s, 0, 95), sm[:, 1:96], OP.min), (sk, "M1" + s), ("W" + s,), 96)
         V(lambda: v.tensor_tensor_scan(a("MM" + s, 97, 192), a("RMX", 0, 95), a("W" + s, 1, 96), 0.0, OP.add, OP.max), ("W" + s, "RMX"), ("M2" + s,), 96)
@@ -572,17 +606,17 @@ def build(g, core, T, topo, rank):
         V(lambda: ts(a("ASK" + s, 0, 6), a("MM" + s, 96 + 15, 192, 16), a("TH2"), None, OP.is_ge), ("M2" + s, "TH2"), ("ASK" + s,), 6)
         V(lambda: v.tensor_tensor(a("AW" + s, 0, 6), a("ASK" + s, 0, 6), a("WCOL", 0, 6), OP.mult), ("ASK" + s, "WCOL"), ("AW" + s,), 12)
         P(lambda: [(sm[:, 0:96], a("BV"), a("G" + s, 96, 192), True, True)] +
-          [(sm[:, 96:102], a("VEX", 128 * l, 128 * l + 128), a("G" + s, 96 + l, 96 + l + 81, 16), l == 0, l == 15) for l in range(16)] +
           [(sm[:, 128:224], a("MVA"), a("G" + s, 0, 96), True, False), (sm[:, 128:224], a("MVB"), a("G" + s, 96, 192), False, True)],
-          ("BV", "G" + s, "MVA", "MVB") + fam["VEX"], (sk,), 1400)
-        V(lambda: v.tensor_copy(a("S12" + s, 0, 6), sm[:, 96:102]), (sk,), ("S12" + s,), 6)
+          ("BV", "G" + s, "MVA", "MVB"), (sk,), 288)
+        V(lambda: v.tensor_tensor(a("SD" + s), a("D96"), sm[:, 0:96], OP.mult), D96 + (sk,), ("SD" + s,), 96)
+        V(lambda: v.tensor_tensor_scan(a("S12" + s), a("HOLD"), a("SD" + s), 0.0, OP.mult, OP.add), ("SD" + s, "HOLD"), ("S12" + s,), 96)
         for c in range(6):
-            V(lambda c=c: ts(a("EE" + s, 96 * c, 96 * c + 96), sm[:, 0:96], a("S12" + s, c, c + 1), a("AW" + s, c, c + 1), OP.is_equal, OP.mult),
+            V(lambda c=c: ts(a("EE" + s, 96 * c, 96 * c + 96), sm[:, 0:96], a("S12" + s, 16 * c + 15, 16 * c + 16), a("AW" + s, c, c + 1), OP.is_equal, OP.mult),
               (sk, "S12" + s, "AW" + s), ("EE%s.%d" % (s, c),), 96)
         S(lambda: sc.activation(a("DAT" + s), sm[:, 128:224], AF.Copy), (sk,), ("DAT" + s,), 96)
         P(lambda: [(sm[:, 0:96], a("BD"), a("EE" + s, 96 * c, 96 * c + 96), c == 0, c == 5) for c in range(6)],
           ("BD",) + tuple("EE%s.%d" % (s, c) for c in range(6)), (sk,), 576)
-        V(lambda: v.tensor_tensor(a("LS" + s, 0, 6), a("S12" + s, 0, 6), a("DMP", 0, 6), OP.subtract), ("S12" + s, "DMP"), ("LS" + s,), 12)
+        V(lambda: v.tensor_tensor(a("LS" + s, 0, 6), a("S12" + s, 15, 96, 16), a("DMP", 0, 6), OP.subtract), ("S12" + s, "DMP"), ("LS" + s,), 12)
         V(lambda: v.tensor_tensor(a("TT" + s, 0, 6), a("LS" + s, 0, 6), a("ASK" + s, 0, 6), OP.mult), ("LS" + s, "ASK" + s), ("TT" + s,), 12)
         V(lambda: v.tensor_tensor(a("R" + s), a("DW"), sm[:, 0:96], OP.mult), DW + (sk,), ("R" + s,), 96)
         V(lambda: v.tensor_tensor_scan(a("RS" + s), a("HOLD"), a("R" + s), 0.0, OP.mult, OP.max), ("R" + s, "HOLD"), ("RS" + s,), 96)
@@ -592,25 +626,29 @@ def build(g, core, T, topo, rank):
         V(lambda: v.tensor_copy(a("SL" + s, 0, 6), a("RS" + s, 0, 6)), ("RS" + s,), ("SL" + s,), 6)
         add("V", lambda: v.tensor_copy(T.tab[:].indirect(a("SL" + s, 0, 6)), a("DAT" + s)), ("SL" + s, "DAT" + s) + tuple(rows), ("tab",), 0.4)
 
-    for ch in (1, 0):
-        state[(0, ch)] = pre(0, ch)
+    def both(stage, t):
+        for ch in (1, 0):
+            now[0] = ch
+            r = stage(t, ch)
+            if stage == pre:
+                state[(t, ch)] = r
+        now[0] = 0
+
+    both(pre, 0)
     for t in range(NV):
-        for stage in (parents, dependent):
-            for ch in (1, 0):
-                stage(t, ch)
+        both(parents, t)
+        both(dependent, t)
         if t < NV - 1:
             counter(t)
-        for ch in (1, 0):
-            truth(t, ch)
-        for ch in (1, 0):
-            asks(t, ch)
+        both(names_leave, t)
+        both(truth, t)
+        both(asks, t)
         if t < NV - 1:
-            for ch in (1, 0):
-                state[(t + 1, ch)] = pre(t + 1, ch)
+            both(pre, t + 1)
     for ch in (1, 0):
-        b, lo = "in%d_%d" % (NV, ch), NC * ch
-        V(lambda b=b, ch=ch: v.tensor_copy(T["yv_s%d" % ch][:], T[b][:, 0:96]), (b,), ("yvs%d" % ch,), 96)
-        V(lambda b=b, ch=ch: v.tensor_copy(T["ye_s%d" % ch][:], T[b][:, 96:192]), (b,), ("yes%d" % ch,), 96)
+        bv, by, lo = "inv%d_%d" % (NV, ch), "iny%d_%d" % (NV, ch), NC * ch
+        V(lambda bv=bv, ch=ch: v.tensor_copy(T["yv_s%d" % ch][:], T[bv][:]), (bv,), ("yvs%d" % ch,), 96)
+        V(lambda by=by, ch=ch: ts(T["ye_s%d" % ch][:], T[by][:], 0.5, None, OP.mult), (by,), ("yes%d" % ch,), 96)
         dma(lambda ch=ch, lo=lo: g.sync.dma_start(T.yv[:, lo:lo + NC], T["yv_s%d" % ch][:]), ("yvs%d" % ch,), ("yv%d" % ch,))
         dma(lambda ch=ch, lo=lo: g.sync.dma_start(T.ye[:, lo:lo + NC], T["ye_s%d" % ch][:]), ("yes%d" % ch,), ("ye%d" % ch,))
     P(lambda: [(T.bg0_0[:, 0:256], a("PEX", 128 * c, 128 * c + 128), T.tab[:, 256 * c:256 * c + 256], c == 0, c == 15) for c in range(16)],

import numpy as np
import comms_topo
from concourse.mybir import dt, AluOpType, AxisListType, ActivationFunctionType

OP = AluOpType
AF = ActivationFunctionType
NV, NC, STEP = 4, 96, 5
CW = 8432

TILES = {}
SIZE = {"bf": 0, "f": 0, "i": 0, "u": 0}
_al = {"bf": 16, "f": 8, "i": 8, "u": 16}


def _tile(kind, name, n):
    TILES[name] = (kind, SIZE[kind], n)
    a = _al[kind]
    SIZE[kind] += (n + a - 1) // a * a


for _p in range(2):
    for _c in range(2):
        _s = "%d%d" % (_p, _c)
        for _n, _w in (("X", 1536), ("PR", 1536), ("D", 1536), ("A", 1536), ("S1", 512 * 3), ("S2", 512 * 3), ("DEP", 96), ("CAN", 96),
                       ("MT", 128), ("YG", 96), ("YT", 128), ("G", 192), ("EE", 576), ("DAT", 96), ("YB", 96)):
            _tile("bf", _n + _s, _w)
        for _n, _w in (("UP", 96), ("VF", 96), ("UH", 96), ("DV", 96), ("VT", 96), ("VN", 96), ("M", 96), ("MM", 192), ("W", 96), ("ASK", 8),
                       ("AW", 8), ("R", 96), ("RS", 96), ("TT", 8), ("WN", 8), ("LS", 8), ("L2", 8), ("S12", 96), ("SD", 96), ("YS", 96)):
            _tile("f", _n + _s, _w)
        for _n, _w in (("UI", 96), ("UJ", 96), ("T1", 96), ("T2", 96), ("T3", 96), ("Q1", 96), ("Q2", 96), ("Q3", 96), ("I1", 8), ("I2", 8),
                       ("E1", 16), ("E2", 16)):
            _tile("i", _n + _s, _w)
        for _n, _w in (("XL", 96), ("ZL", 96), ("VL", 96), ("YL", 16), ("AB", 16), ("SL", 16)):
            _tile("u", _n + _s, _w)
for _n, _w in (("I128", 128), ("TL", 128), ("TI", 128), ("BD", 128), ("WBD", 128), ("BV", 128), ("SUM", 2048), ("WTL", 2048), ("PEX", 2048),
               ("VEX", 2048), ("EXP", 2048), ("ONE", 128), ("HALF", 1536), ("EM0", 1536), ("EM1", 1536), ("EY0", 1536), ("EY1", 1536), ("PERM", 96),
               ("CA", 96), ("CB", 128), ("H96", 96), ("C1a", 96), ("C2a", 96), ("N1a", 96), ("N2a", 96), ("C1b", 96), ("C2b", 96), ("N1b", 96), ("N2b", 96),
               ("RMX", 512), ("RMN", 512), ("HOLD", 96), ("MVA", 128), ("MVB", 128), ("MVT", 128), ("SELT", 128), ("Z96", 96), ("P23", 128), ("IHL", 1024),
               ("D16", 16), ("L16", 16), ("PEN", 128)):
    _tile("bf", _n, _w)
for _n, _w in (("MODP", 1), ("WTF", 1), ("COLP", 1), ("COLV", 1), ("C23", 1), ("NM", 8), ("ca", 1), ("cb", 1), ("cc", 1), ("M96", 1), ("THF", 8),
               ("THC1", 1), ("THC2", 1), ("THC3", 1), ("TH2", 1), ("CNT1", 1), ("CNT2", 1), ("CNT3", 1), ("LIMF", 8), ("T8", 128), ("PW", 96),
               ("PH", 96), ("WCOL", 8), ("WINV", 8), ("LI96", 96), ("DL", 96), ("WZ", 96), ("WA", 48), ("WB", 24), ("WC", 16), ("DW", 96), ("D96", 96), ("DMP", 8),
               ("DMI", 8), ("YPF", 256), ("LO8", 8)):
    _tile("f", _n, _w)
for _n, _w in (("PI", 1), ("PJ", 1), ("CN1", 1), ("CN2", 1), ("CN3", 1), ("CM1", 1), ("CM2", 1), ("CM3", 1), ("IH", 512), ("IL", 512)):
    _tile("i", _n, _w)

SCRATCH = {
    "bf": ("sbuf", [128, SIZE["bf"]], "bfloat16"), "f": ("sbuf", [128, SIZE["f"]], "float32"),
    "i": ("sbuf", [128, SIZE["i"]], "int32"), "u": ("sbuf", [128, SIZE["u"]], "uint16"),
    "clm": ("sbuf", [128, CW], "bfloat16"), "tab": ("sbuf", [128, 4192], "bfloat16"),
    "who_s": ("sbuf", [128, 192], "int32"), "est_s": ("sbuf", [128, 192], "bfloat16"), "wt_s": ("sbuf", [128, 1], "int32"),
    "lim_s": ("sbuf", [8, 2], "int32"), "par_s": ("sbuf", [128, 256], "int32"), "ids_s": ("sbuf", [128, 256], "int32"),
    "yv_s0": ("sbuf", [128, 96], "float32"), "ye_s0": ("sbuf", [128, 96], "bfloat16"),
    "yv_s1": ("sbuf", [128, 96], "float32"), "ye_s1": ("sbuf", [128, 96], "bfloat16"),
}
for _c in range(2):
    for _t in range(1, 5):
        for _n in ("inv", "iny", "outv", "outy"):
            SCRATCH["%s%d_%d" % (_n, _t, _c)] = ("sbuf", [128, 96], "uint16")
    for _n in ("pre%d" % _c, "sm%d" % _c, "bg%d_0" % _c, "bg%d_1" % _c):
        SCRATCH[_n] = ("psum", [128, 512], "float32")
NLD = 20
WHO = {"%s%d%d%d" % (_n, _v, _c, _b): "A" for _n in "XP" for _v in range(2) for _c in range(2) for _b in range(3)}
WHO.update({"F%d%d" % (_c, _b): "A" for _c in range(2) for _b in range(3)})
WHO.update({_n: "V" for _n in ("F01", "F02", "F10", "F12", "P000", "P001", "P002", "P010", "P110", "P112")})
PECY = 0.00042
SCOPY = (("S1", 0), ("S2", 0))
FARV = (("M", 0),)
HOP = 0.1
FIXV, FIXA = 0.02, 0.02
LEAD = 2.0
SEMAPHORES = ["qV", "qA", "qP", "qG", "snt"] + ["ld%d" % k for k in range(NLD)] + ["arr%s%d_%d" % (x, t, c) for x in "vy" for t in range(1, 5) for c in range(2)]


def route(T, topo, rank, t, ch):
    n = len(T.cores)
    src = T.cores[rank]
    dst = T.cores[(rank + (STEP if t < NV else -STEP * (NV - 1))) % n]
    if topo.may_write(src, dst):
        return [src, dst]
    via = [h for h in topo.cores_of(src) if h != src and topo.die(h) == topo.die(src) and topo.may_write(h, dst)]
    return [src, via[ch % len(via)], dst]


def send(g, T, topo, src, dst, out, in_, arr):
    rid, pid = topo.addr(dst, src)
    g.remote_dma(out_ap=out, in_ap=in_, remote_sem=T.sem[arr], local_sem=T.sem["snt"], pid=pid, routing_id=rid, dma_engine_mask=topo.mask(src, dst))
    return len(topo.engines(src, dst))


def helper_program(g, core, T, topo):
    left, legs = 0, []
    for t in range(1, NV + 1):
        for ch in (1, 0):
            for r in range(len(T.cores)):
                way = route(T, topo, r, t, ch)
                if len(way) == 3 and way[1] == core:
                    legs += [(t, x == "y", 1 - ch, "in%s%d_%d" % (x, t, ch), "arr%s%d_%d" % (x, t, ch), way) for x in "vy"]
    for _, _, _, b, a, way in sorted(legs):
        g.wait_ge(T.sem[a], len(topo.engines(way[0], core)))
        left += send(g, T, topo, core, way[2], T[b][:], T[b][:], a)
    if left:
        g.wait_ge(T.sem["snt"], left)


def rank_program(g, core, T, topo):
    rank = T.rank_of(core)
    if rank is None:
        helper_program(g, core, T, topo)
        return
    prog = build(g, core, T, topo, rank)
    emit(g, T, prog, schedule(prog))


def schedule(ops):
    n = len(ops)
    succ = [[] for _ in range(n)]
    for k, o in enumerate(ops):
        for d in o["deps"]:
            succ[d].append(k)
    low = [0.0] * n
    for k in range(n - 1, -1, -1):
        low[k] = ops[k]["cost"] + ops[k]["lat"] + HOP + max([low[s] for s in succ[k]] + [0.0])
    for k in range(n):
        low[k] += LEAD * ops[k]["ch"] + ops[k]["pri"]
    need = [len(o["deps"]) for o in ops]
    ready = [0.0] * n
    avail = {}
    free = {}
    for k in range(n):
        avail.setdefault(ops[k]["q"], [])
        free[ops[k]["q"]] = 0.0
        if not need[k]:
            avail[ops[k]["q"]].append(k)
    order = {q: [] for q in avail}
    done = 0
    while done < n:
        best = None
        for q in avail:
            if not avail[q]:
                continue
            t0 = max(free[q], min(ready[k] for k in avail[q]))
            if best is None or t0 < best[0]:
                best = (t0, q)
        t0, q = best
        cand = [k for k in avail[q] if ready[k] <= t0 + 1e-9]
        k = max(cand, key=lambda x: (low[x], -x))
        avail[q].remove(k)
        order[q].append(k)
        free[q] = t0 + ops[k]["cost"]
        end = free[q] + ops[k]["lat"]
        for s in succ[k]:
            need[s] -= 1
            ready[s] = max(ready[s], end + HOP)
            if not need[s]:
                avail[ops[s]["q"]].append(s)
        done += 1
    return order


def emit(g, T, ops, order):
    n = len(ops)
    count = {}
    tok = [None] * n
    nld = [0]
    for q in order:
        for k in order[q]:
            o = ops[k]
            if o["kind"] == "dma":
                tok[k] = ("ld%d" % nld[0], 16)
                nld[0] += 1
            elif o["kind"] == "recv":
                tok[k] = o["tok"]
            elif o["kind"] == "send":
                tok[k] = None
            else:
                count[q] = count.get(q, 0) + 1
                tok[k] = ("q" + q, count[q])
    pos = {q: 0 for q in order}
    engine = {"V": g.vector, "A": g.scalar, "P": g.tensor, "G": g, "S": g.sync}
    seen = {q: {} for q in order}
    clock = [None] * n
    left = n
    while left:
        moved = False
        for q in order:
            while pos[q] < len(order[q]):
                k = order[q][pos[q]]
                o = ops[k]
                if any(clock[d] is None for d in o["deps"]):
                    break
                if o["kind"] == "recv":
                    clock[k] = {tok[k][0]: tok[k][1]}
                else:
                    mine = seen[q]
                    for d in sorted(o["deps"], reverse=True):
                        if tok[d] is None:
                            continue
                        s, v = tok[d]
                        if mine.get(s, 0) < v:
                            engine[q].wait_ge(T.sem[s], v)
                            for s2, v2 in clock[d].items():
                                if mine.get(s2, 0) < v2:
                                    mine[s2] = v2
                    ins = o["fn"]()
                    if o["kind"] == "dma":
                        ins.then_inc(T.sem[tok[k][0]], 16)
                    elif o["kind"] == "op":
                        ins.then_inc(T.sem[tok[k][0]], 1)
                    clock[k] = dict(mine)
                    if tok[k]:
                        clock[k][tok[k][0]] = tok[k][1]
                pos[q] += 1
                left -= 1
                moved = True
        if not moved:
            raise ValueError("order")
    mine = seen["G"]
    last = {}
    for k in range(n):
        if tok[k] and mine.get(tok[k][0], 0) < tok[k][1]:
            last[tok[k][0]] = max(last.get(tok[k][0], 0), tok[k][1])
    for s in last:
        g.wait_ge(T.sem[s], last[s])
    g.wait_ge(T.sem["snt"], sum(o["sent"] for o in ops))


def build(g, core, T, topo, rank):
    ops = []
    wr, rd = {}, {}
    now = [0]

    def add(q, fn, r=(), w=(), cost=0.1, lat=0.0, kind="op", tok=None, sent=0):
        k = len(ops)
        deps = set()
        for x in r:
            deps.update(wr.get(x, []))
            if x[0] == "#":
                deps.update(d for d in rd.get(x, []) if ops[d]["q"] != q)
        for x in w:
            deps.update(wr.get(x, []))
            deps.update(rd.get(x, []))
        for x in r:
            rd.setdefault(x, []).append(k)
        for x in w:
            wr[x] = [k]
            rd[x] = []
        deps.discard(k)
        ops.append({"q": q, "fn": fn, "nm": (tuple(w) + ("",))[0], "deps": sorted(deps), "ch": now[0], "pri": 0.0, "cost": cost, "lat": lat, "kind": kind, "tok": tok, "sent": sent})
        return k

    def a(name, lo=0, hi=None, st=1, p=128):
        kind, off, n = TILES[name]
        hi = n if hi is None else hi
        return T[kind][0:p, off + lo:off + hi:st] if st > 1 else T[kind][0:p, off + lo:off + hi]

    def col(name, c=0):
        return a(name, c, c + 1)

    cyc = 0.00083

    def V(fn, r, w, n):
        return add("V", fn, r, w, FIXV + max(64, n) * cyc)

    def S(fn, r, w, n):
        return add("A", fn, r, w, FIXA + max(64, n) * cyc)

    def copy(q, out, in_, r, w, cost, scale=None):
        def fn():
            if q == "A":
                return g.scalar.activation(out(), in_(), AF.Copy) if scale is None else g.scalar.activation(out(), in_(), AF.Copy, scale=scale)
            return g.vector.tensor_copy(out(), in_()) if scale is None else g.vector.tensor_scalar(out(), in_(), scale, None, OP.mult)
        return add(q, fn, r, w, cost)

    def P(mms, r, w, cycles):
        def fn():
            ins = None
            for m in mms():
                ins = g.tensor.matmul(*m)
            return ins
        return add("P", fn, r, w, cycles * PECY)

    def G(fn, r, w, n):
        return add("G", fn, r, w, 0.17 + 2 * n * cyc)

    def dma(fn, r, w, q="S", cost=0.1, lat=2.5):
        return add(q, fn, r, w, cost, lat, kind="dma")

    v, sc = g.vector, g.scalar
    GATHER = 0.065 + 512 * 1.5 * cyc

    dma(lambda: g.sync.dma_start(T.who_s[:], T.who[:]), (), ("who_s",))
    dma(lambda: g.sync.dma_start(T.wt_s[:], T.wt[:]), (), ("wt_s",))
    dma(lambda: g.sync.dma_start(T.est_s[:], T.est[:]), (), ("est_s",))
    dma(lambda: g.sync.dma_start(T.par_s[:], T.par[:]), (), ("par_s",))
    dma(lambda: g.sync.dma_start(T.lim_s[:], T.lim[:]), (), ("lim_s",))
    dma(lambda: g.scalar.dma_start(T.clm[:, 0:4096], T.claim[:]), (), ("clm0",), q="A", lat=6.0)
    dma(lambda: g.scalar.dma_start(T.clm[:, 4096:8192], T.claim[:]), (), ("clm1",), q="A", lat=9.0)
    dma(lambda: g.scalar.dma_start(T.clm[:, 8192:CW], T.claim[:, 0:CW - 8192]), (), ("clm2",), q="A", lat=9.0)
    CLM = ("clm0", "clm1", "clm2")

    def ts(out, in0, s1, s2, o0, o1=None):
        return v.tensor_scalar(out, in0, s1, s2, o0) if o1 is None else v.tensor_scalar(out, in0, s1, s2, o0, o1)

    G(lambda: g.iota(a("PI"), [[0, 1]], 0, 1), (), ("PI",), 1)
    V(lambda: ts(a("PJ"), a("PI"), 15, None, OP.bitwise_and), ("PI",), ("PJ",), 1)
    V(lambda: v.tensor_copy(a("MODP"), a("PJ")), ("PJ",), ("MODP",), 1)
    for c, (x, s) in enumerate(((0, 16.0), (1, 1.0), (2, 16.0), (3, 1.0))):
        V(lambda c=c, x=x, s=s: ts(a("NM", c, c + 1), a("MODP"), float(x), s, OP.is_equal, OP.mult), ("MODP",), ("NM%d" % c,), 1)
    V(lambda: v.tensor_tensor(a("COLP"), a("NM", 0, 1), a("NM", 1, 2), OP.add), ("NM0", "NM1"), ("COLP",), 1)
    V(lambda: v.tensor_tensor(a("COLV"), a("NM", 2, 3), a("NM", 3, 4), OP.add), ("NM2", "NM3"), ("COLV",), 1)
    V(lambda: ts(a("C23"), a("COLV"), 0.5, None, OP.is_gt), ("COLV",), ("C23",), 1)
    V(lambda: v.tensor_copy(a("WTF"), T.wt_s[:]), ("wt_s",), ("WTF",), 1)
    G(lambda: g.iota(a("TI"), [[-16, 8], [0, 16]], 0, 1, allow_small_or_imprecise_dtypes=True), (), ("TI",), 128)
    G(lambda: g.iota(a("MVT"), [[0, 8], [1, 16]], 0, 0, allow_small_or_imprecise_dtypes=True), (), ("MVT",), 128)
    G(lambda: g.affine_select(a("SELT"), a("MVT"), [[-16, 8], [0, 16]], OP.is_ge, -1.0, 0, 1), ("MVT",), ("SELT",), 128)
    G(lambda: g.affine_select(a("TL"), a("SELT"), [[16, 8], [0, 16]], OP.is_ge, -1.0, 15, -1), ("SELT",), ("TL",), 128)
    V(lambda: v.memset(a("ONE"), 1.0), (), ("ONE",), 64)
    G(lambda: g.affine_select(a("I128"), a("ONE"), [[-1, 128]], OP.is_equal, 0.0, 0, 1), ("ONE",), ("I128",), 128)
    V(lambda: ts(a("BD"), a("TL"), 0.0, None, OP.is_ge), ("TL",), ("BD",), 64)
    V(lambda: ts(a("WBD"), a("BD"), a("WTF"), None, OP.mult), ("BD", "WTF"), ("WBD",), 64)
    V(lambda: ts(a("BV"), a("BD"), a("COLV"), None, OP.mult), ("BD", "COLV"), ("BV",), 64)
    for l in range(16):
        lo, hi = 128 * l, 128 * l + 128
        V(lambda l=l, lo=lo, hi=hi: ts(a("SUM", lo, hi), a("TL"), float(l), None, OP.is_equal), ("TL",), ("SUM.%d" % l,), 64)
        V(lambda l=l, lo=lo, hi=hi: ts(a("EXP", lo, hi), a("TI"), float(l), -256.0, OP.is_equal, OP.mult), ("TI",), ("EXP.%d" % l,), 64)
    fam = {f: tuple("%s.%d" % (f, l) for l in range(16)) for f in ("SUM", "EXP")}
    fam.update({f: tuple("%s.%d" % (f, h) for h in range(2)) for f in ("WTL", "PEX", "VEX")})
    for f, c in (("PEX", "COLP"), ("VEX", "COLV"), ("WTL", "WTF")):
        for h in range(2):
            S(lambda f=f, c=c, h=h: sc.activation(a(f, 1024 * h, 1024 * h + 1024), a("SUM", 1024 * h, 1024 * h + 1024), AF.Copy, scale=a(c)),
              (c,) + fam["SUM"][8 * h:8 * h + 8], ("%s.%d" % (f, h),), 1024)
    V(lambda: v.memset(a("HALF"), -0.5), (), ("HALF",), 768)
    sel = lambda out, pat, key, n: G(lambda: g.affine_select(a(out, p=96), a("HALF", 0, n, p=96), pat, OP.is_equal, 0.0, 0, 1), ("HALF",), (key,), n)
    sel("EM0", [[-1, 96], [0, 16]], "EM0", 1536)
    sel("PERM", [[-1, 16], [-16, 6]], "PERM", 96)
    sel("EY0", [[-1, 16], [-16, 6], [0, 16]], "EY0", 1536)
    sel("EM1", [[-1, 6], [0, 16], [-6, 16]], "EM1", 1536)
    sel("EY1", [[-16, 6], [0, 16], [-1, 16]], "EY1", 1536)
    V(lambda: v.memset(a("CA"), 0.4375), (), ("CA",), 64)
    V(lambda: v.memset(a("CB"), 4.5625), (), ("CB",), 64)
    flat = lambda out, n, x=0: G(lambda: g.iota(a(out), [[0, n]], x, 0, allow_small_or_imprecise_dtypes=True), (), (out,), n)
    V(lambda: v.memset(a("H96"), 0.5), (), ("H96",), 64)
    flat("Z96", 96)
    G(lambda: g.iota(a("C1a"), [[16, 6], [1, 16]], 0, 0, allow_small_or_imprecise_dtypes=True), (), ("C1a",), 96)
    V(lambda: ts(a("M96"), a("MODP"), 96.0, None, OP.mult), ("MODP",), ("M96",), 1)
    V(lambda: ts(a("C2a"), a("Z96"), a("M96"), None, OP.add), ("Z96", "M96"), ("C2a",), 64)
    V(lambda: ts(a("N1a"), a("C1a"), -1.0, -1.0, OP.mult, OP.add), ("C1a",), ("N1a",), 64)
    V(lambda: ts(a("N2a"), a("C2a"), -1.0, 2048.0, OP.mult, OP.add), ("C2a",), ("N2a",), 64)
    V(lambda: ts(a("C1b"), a("C1a"), 16.0, None, OP.mult), ("C1a",), ("C1b",), 64)
    V(lambda: ts(a("C2b"), a("Z96"), a("MODP"), None, OP.add), ("Z96", "MODP"), ("C2b",), 64)
    V(lambda: ts(a("N1b"), a("C1b"), -1.0, 2048.0, OP.mult, OP.add), ("C1b",), ("N1b",), 64)
    V(lambda: ts(a("N2b"), a("C2b"), -1.0, -1.0, OP.mult, OP.add), ("C2b",), ("N2b",), 64)
    V(lambda: ts(a("PEN"), a("I128"), float(2 ** 23), None, OP.mult), ("I128",), ("PEN",), 64)
    BIG = float(2 ** 30)
    flat("RMX", 512)
    G(lambda: g.affine_select(a("RMX"), a("RMX"), [[0, 32], [1, 16]], OP.not_equal, -BIG, 0, 0), ("RMX",), ("RMX",), 512)
    S(lambda: sc.activation(a("RMN"), a("RMX"), AF.Copy, scale=-1.0), ("RMX",), ("RMN",), 512)
    flat("HOLD", 96, 1)
    G(lambda: g.affine_select(a("HOLD"), a("HOLD"), [[0, 6], [1, 16]], OP.not_equal, 0.0, 0, 0), ("HOLD",), ("HOLD",), 96)
    for s in ("00", "01", "10", "11"):
        flat("UH" + s, 96)
    G(lambda: g.affine_select(a("P23"), a("ONE"), [[-1, 128]], OP.is_equal, 0.0, -2, 1), ("ONE",), ("P23",), 128)
    V(lambda: ts(a("MVA"), a("P23"), a("C23"), None, OP.mult), ("P23", "C23"), ("MVA",), 64)
    V(lambda: ts(a("MVB"), a("I128"), a("C23"), None, OP.mult), ("I128", "C23"), ("MVB",), 64)
    V(lambda: v.memset(a("PH"), 0.5), (), ("PH",), 96)
    G(lambda: g.iota(a("LI96"), [[1, 16], [0, 6]], 0, 0, allow_small_or_imprecise_dtypes=True), (), ("LI96",), 96)
    V(lambda: v.tensor_tensor_scan(a("PW"), a("PH"), a("Z96"), float(2 ** 49), OP.mult, OP.max), ("PH", "Z96"), ("PW",), 96)
    V(lambda: ts(a("DL"), a("LI96"), a("MODP"), None, OP.is_equal), ("LI96", "MODP"), ("DL",), 96)
    V(lambda: v.tensor_tensor(a("WZ"), a("DL"), a("PW"), OP.mult), ("DL", "PW"), ("WZ",), 192)
    for src, dst, n in (("WZ", "WA", 48), ("WA", "WB", 24), ("WB", "WC", 12), ("WC", "WCOL", 6)):
        V(lambda src=src, dst=dst, n=n: v.tensor_tensor(a(dst, 0, n), a(src, 0, n), a(src, n, 2 * n), OP.add), (src,), (dst,), 96)
    V(lambda: v.reciprocal(a("WINV", 0, 6), a("WCOL", 0, 6)), ("WCOL",), ("WINV",), 300)
    G(lambda: g.iota(a("L16"), [[1, 16]], 0, 0, allow_small_or_imprecise_dtypes=True), (), ("L16",), 16)
    for c in range(6):
        V(lambda c=c: ts(a("DW", 16 * c, 16 * c + 16), a("L16"), a("MODP"), a("WINV", c, c + 1), OP.is_equal, OP.mult), ("L16", "MODP", "WINV"), ("DW%d" % c,), 16)
        V(lambda c=c: ts(a("D96", 16 * c, 16 * c + 16), a("L16"), a("MODP"), None, OP.is_equal), ("L16", "MODP"), ("D96.%d" % c,), 16)
    DW = tuple("DW%d" % c for c in range(6))
    D96 = tuple("D96.%d" % c for c in range(6))
    G(lambda: g.iota(a("DMI", 0, 6), [[16, 6]], 4096, 0, allow_small_or_imprecise_dtypes=True), (), ("DMI",), 6)
    V(lambda: ts(a("DMP", 0, 6), a("DMI", 0, 6), a("MODP"), None, OP.add), ("DMI", "MODP"), ("DMP",), 6)
    V(lambda: v.tensor_copy(a("LIMF", 0, 2, p=8), T.lim_s[:]), ("lim_s",), ("LIMF",), 2)
    V(lambda: v.memset(a("T8", p=8), 1.0), (), ("T8a",), 128)
    G(lambda: g.affine_select(a("T8", p=8), a("T8", p=8), [[-1, 8], [0, 16]], OP.is_equal, 0.0, 0, 1), ("T8a",), ("T8", "T8a"), 128)
    P(lambda: [(T.pre1[:, 0:2], a("T8", p=8), a("LIMF", 0, 2, p=8), True, True)], ("T8", "LIMF"), ("#pre1",), 256)
    V(lambda: v.tensor_copy(a("THF", 0, 2), T.pre1[:, 0:2]), ("#pre1",), ("THF",), 2)
    V(lambda: ts(a("TH2"), a("THF", 1, 2), 2048.0, None, OP.mult), ("THF",), ("TH2",), 1)
    G(lambda: g.iota(T.ids_s[:], [[1, 256]], 0, 256), (), ("ids_s",), 256)
    for h, (src, o) in enumerate(((("par_s"), 0), (("ids_s"), 256))):
        V(lambda src=src, o=o: ts(a("IH", o, o + 256), T[src][:], 4, 255, OP.logical_shift_right, OP.bitwise_and), (src,), ("IH%d" % h,), 256)
        V(lambda src=src, o=o: ts(a("IL", o, o + 256), T[src][:], 15, None, OP.bitwise_and), (src,), ("IL%d" % h,), 256)
        V(lambda o=o: v.tensor_copy(a("IHL", o, o + 256), a("IH", o, o + 256)), ("IH%d" % h,), ("IHLh%d" % h,), 256)
        V(lambda o=o: v.tensor_copy(a("IHL", 512 + o, 512 + o + 256), a("IL", o, o + 256)), ("IL%d" % h,), ("IHLl%d" % h,), 256)
    V(lambda: v.memset(T.tab[:], 0.0), (), ("tab",), 2096)
    for r, (o, key) in enumerate(((0, "IHLh0"), (512, "IHLl0"), (256, "IHLh1"), (768, "IHLl1"))):
        k = dma(lambda r=r, o=o: g.sync.dma_start(T.tab[r::16, 0:4096], a("IHL", o, o + 256)), (key, "tab"), ("tabr%d" % r,))
    rows = ["tabr%d" % r for r in range(4)]

    def mod(t, ch):
        return t % 2

    def pre(t, ch):
        s = "%d%d" % (t % 2, ch)
        pb, pk = T["pre%d" % ch], "#pre%d" % ch
        lo = NC * ch
        if t == 0:
            yb, ykey = T.est_s[:, lo:lo + NC], "est_s"
            vf, vkey = T.who_s[:, lo:lo + NC], "who_s"
            V(lambda: v.tensor_copy(a("VL" + s), vf), (vkey,), ("VL" + s,), 96)
            vl, lkey = a("VL" + s), "VL" + s
            P(lambda: [(pb[:, 0:96], a("WBD"), yb, True, True)], ("WBD", ykey), (pk,), 96)
            V(lambda: v.tensor_copy(a("UI" + s), pb[:, 0:96]), (pk,), ("UI" + s,), 96)
            V(lambda: ts(a("UJ" + s), a("UI" + s), 4095, None, OP.bitwise_and), ("UI" + s,), ("UJ" + s,), 96)
            up, ukey = a("UJ" + s), "UJ" + s
        else:
            inv, iny, key, key2 = T["inv%d_%d" % (t, ch)], T["iny%d_%d" % (t, ch)], "inv%d_%d" % (t, ch), "iny%d_%d" % (t, ch)
            V(lambda: ts(a("YB" + s), iny[:], 0.5, None, OP.mult), (key2,), ("YB" + s,), 48)
            V(lambda: v.tensor_copy(a("VF" + s), inv[:]), (key,), ("VF" + s,), 96)
            vf, vkey, vl, lkey, yb, ykey = a("VF" + s), "VF" + s, inv[:], key, a("YB" + s), "YB" + s
            P(lambda: [(pb[:, 0:6], a("WTL", 128 * l, 128 * l + 128), a("YB" + s, 6 * l, 6 * l + 6), l == 0, l == 15) for l in range(16)],
              fam["WTL"] + (ykey,), (pk,), 1024)
            V(lambda: v.tensor_copy(a("UI" + s, 0, 6), pb[:, 0:6]), (pk,), ("UI" + s,), 6)
            V(lambda: ts(a("UJ" + s, 0, 6), a("UI" + s, 0, 6), 4095, None, OP.bitwise_and), ("UI" + s,), ("UJ" + s,), 6)
            V(lambda: v.tensor_copy(a("UH" + s, 0, 96, 16), a("UJ" + s, 0, 6)), ("UJ" + s,), ("UH" + s,), 6)
            V(lambda: v.tensor_tensor_scan(a("UP" + s), a("HOLD"), a("UH" + s), 0.0, OP.mult, OP.add), ("HOLD", "UH" + s), ("UP" + s,), 96)
            up, ukey = a("UP" + s), "UP" + s
        hash_(t, s, "T", vf, vkey, 192, up, ukey, "XL")
        for b in range(3):
            copy(WHO["X%d%d%d" % (min(t, 1), ch, b)], lambda b=b: a("X" + s, 512 * b, 512 * b + 512), lambda b=b: T.clm[:].indirect(a("XL" + s, 32 * b, 32 * b + 32)),
                 ("XL" + s,) + CLM, ("X%s.%d" % (s, b),), GATHER)
        return vf, vkey, vl, lkey, yb, ykey, up, ukey

    def hash_(t, s, x, vf, vkey, n, up, ukey, out):
        V(lambda: v.tensor_tensor(a(x + "1" + s), vf, up, OP.mult), (vkey, ukey), (x + "1" + s,), n)
        V(lambda: ts(a(x + "2" + s), a(x + "1" + s), 5, 4095, OP.logical_shift_right, OP.bitwise_and), (x + "1" + s,), (x + "2" + s,), 96)
        V(lambda: v.tensor_tensor(a(x + "3" + s), vf, a(x + "2" + s), OP.add), (vkey, x + "2" + s), (x + "3" + s,), n)
        V(lambda: ts(a(out + s), a(x + "3" + s), 77 * t, None, OP.add), (x + "3" + s,), (out + s,), 96)

    def sl(name, t, l, n0=0, n1=96):
        if t == 0:
            return a(name, 96 * l + n0, 96 * l + n1)
        return a(name, 16 * n0 + l, 16 * (n1 - 1) + l + 1, 16)

    def psum_P(out, f, name, t, r):
        return [(out, a(f, 128 * l, 128 * l + 128), sl(name, t, l), l == 0, l == 15) for l in range(16)]

    b3 = lambda name: tuple("%s.%d" % (name, b) for b in range(3))
    state = {}

    def parents(t, ch):
        s = "%d%d" % (t % 2, ch)
        vf, vkey, vl, lkey, yb, ykey, up, ukey = state[(t, ch)]
        pb, pk, sm, sk = T["pre%d" % ch], "#pre%d" % ch, T["sm%d" % ch], "#sm%d" % ch
        for b in range(3):
            copy(WHO["P%d%d%d" % (min(t, 1), ch, b)], lambda b=b: a("PR" + s, 512 * b, 512 * b + 512), lambda b=b: T.tab[:, 0:4096].indirect(lst(t, ch, s, b)),
                 (lkey, "tab") + tuple(rows), ("PR%s.%d" % (s, b),), GATHER)
        if t == 0:
            P(lambda: [(pb[:, 0:96], a("PEX", 128 * k, 128 * k + 128), a("PR" + s, k, 1536 - 15 + k, 16), k == 0, k == 15) for k in range(16)],
              fam["PEX"] + b3("PR" + s), (pk,), 1536)
            hash_(t, s, "Q", pb[:, 0:96], pk, 96, up, ukey, "ZL")
            P(lambda: psum_P(sm[:, 0:96], "VEX", "PR" + s, t, 0), fam["VEX"] + b3("PR" + s), (sk,), 1536)
            V(lambda: v.tensor_copy(a("VF" + s), sm[:, 0:96]), (sk,), ("VF" + s,), 96)
            P(lambda: psum_P(sm[:, 0:96], "PEX", "PR" + s, t, 0), fam["PEX"] + b3("PR" + s), (sk,), 1536)
            V(lambda: v.tensor_tensor(a("DV" + s), sm[:, 0:96], a("VF" + s), OP.subtract), (sk, "VF" + s), ("DV" + s,), 96)
        else:
            P(lambda: psum_P(sm[:, 0:96], "PEX", "PR" + s, t, 0), fam["PEX"] + b3("PR" + s), (sk,), 1536)
            hash_(t, s, "Q", sm[:, 0:96], sk, 96, up, ukey, "ZL")
            V(lambda: v.tensor_tensor(a("DV" + s), sm[:, 0:96], a("VF" + s), OP.subtract), (sk, "VF" + s), ("DV" + s,), 96)
        for b in range(3):
            x = (512 * b, 512 * b + 512)
            add("V", lambda b=b, x=x: v.tensor_tensor(a("D" + s, *x), T.clm[:].indirect(a("ZL" + s, 32 * b, 32 * b + 32)), a("X" + s, *x), OP.subtract),
                ("ZL" + s, "X%s.%d" % (s, b)) + CLM, ("D%s.%d" % (s, b),), 0.05 + 512 * 1.5 * cyc)
            S(lambda x=x: sc.activation(a("A" + s, *x), a("D" + s, *x), AF.Abs), ("D%s.%d" % (s, b),), ("A%s.%d" % (s, b),), 512)

    def lst(t, ch, s, b):
        return a("VL" + s, 32 * b, 32 * b + 32) if t == 0 else T["inv%d_%d" % (t, ch)][:, 32 * b:32 * b + 32]

    def dependent(t, ch):
        s = "%d%d" % (t % 2, ch)
        sm, sk = T["sm%d" % ch], "#sm%d" % ch
        th, tkey = (a("THF", 0, 1), "THF") if t == 0 else (a("THC%d" % t), "THC%d" % t)
        P(lambda: psum_P(sm[:, 0:96], "SUM", "A" + s, t, 0), fam["SUM"] + b3("A" + s), (sk,), 1536)
        V(lambda: ts(a("DEP" + s), sm[:, 0:96], th, None, OP.is_lt), (sk, tkey), ("DEP" + s,), 96)
        S(lambda: sc.activation(a("CAN" + s), a("DEP" + s), AF.Copy, bias=1.0, scale=-1.0), ("DEP" + s,), ("CAN" + s,), 96)
        for m, out, data0, rkey, op1 in (("DEP", "S1", "RMX", "RMX", OP.max), ("CAN", "S2", "RMN", "RMN", OP.min)):
            for b in range(3):
                bank = "bg%d_%d" % (ch, (b + (m == "CAN")) % 2)

                def mms(b=b, m=m, bank=bank):
                    res = []
                    for l in range(16):
                        lo, hi = max(96 * l, 512 * b), min(96 * l + 96, 512 * b + 512)
                        if lo < hi:
                            o = T[bank][:, lo - 512 * b:hi - 512 * b]
                            n0, n1 = lo - 96 * l, hi - 96 * l
                            res.append((o, a("I128"), sl("X" + s, t, l, n0, n1), True, False))
                            res.append((o, a("EXP", 128 * l, 128 * l + 128), a(m + s, n0, n1), False, True))
                    return res
                P(mms, ("I128", m + s) + fam["EXP"] + b3("X" + s), ("#" + bank,), 1100)
                if (out, b) in SCOPY:
                    S(lambda b=b, bank=bank: sc.activation(a("D" + s, 512 * b, 512 * b + 512), T[bank][:, 0:512], AF.Copy), ("#" + bank,), ("D%s.%d" % (s, b),), 512)
                    V(lambda b=b, out=out, data0=data0, op1=op1: v.tensor_tensor_scan(a(out + s, 512 * b, 512 * b + 512), a(data0), a("D" + s, 512 * b, 512 * b + 512), 0.0, OP.add, op1),
                      ("D%s.%d" % (s, b), rkey), ("%s%s.%d" % (out, s, b),), 256)
                    continue
                V(lambda b=b, out=out, data0=data0, op1=op1, bank=bank: v.tensor_tensor_scan(a(out + s, 512 * b, 512 * b + 512), a(data0), T[bank][:, 0:512], 0.0, OP.add, op1),
                  ("#" + bank, rkey), ("%s%s.%d" % (out, s, b),), 512)
        V(lambda: v.tensor_tensor(a("VT" + s), a("DEP" + s), a("DV" + s), OP.mult), ("DEP" + s, "DV" + s), ("VT" + s,), 192)
        V(lambda: v.tensor_tensor(a("VN" + s), a("VT" + s), a("VF" + s), OP.add), ("VT" + s, "VF" + s), ("VN" + s,), 192)
        ob, ok = T["outv%d_%d" % (t + 1, ch)], "outv%d_%d" % (t + 1, ch)
        if t < NV - 1:
            V(lambda: v.tensor_copy(ob[:], a("VN" + s)), ("VN" + s,), (ok,), 96)
        else:
            V(lambda: v.tensor_copy(a("VL" + s), a("VN" + s)), ("VN" + s,), ("VL" + s,), 96)
            for b in range(3):
                copy(WHO["F%d%d" % (ch, b)], lambda b=b: a("D" + s, 512 * b, 512 * b + 512), lambda b=b: T.tab[:, 0:4096].indirect(a("VL" + s, 32 * b, 32 * b + 32)),
                     ("VL" + s, "tab") + tuple(rows), ("D%s.%d" % (s, b),), GATHER)
            pb, pk = T["pre%d" % ch], "#pre%d" % ch
            for c in range(6):
                P(lambda c=c: [(pb[:, c:c + 91:6], a("VEX", 128 * k, 128 * k + 128), a("D" + s, 256 * c + 16 * k, 256 * c + 16 * k + 16), k == 0, k == 15)
                               for k in range(16)], fam["VEX"] + ("D%s.%d" % (s, c // 2),), (pk,), 1024)
            V(lambda: v.tensor_copy(ob[:], pb[:, 0:96]), (pk,), (ok,), 96)

    def names_leave(t, ch):
        leave("v", t, ch)

    def counter(t):
        s0, s1 = "%d0" % (t % 2), "%d1" % (t % 2)
        n = "%d" % (t + 1)
        P(lambda: [(T.sm0[:, 0:96], a("ONE"), a("DEP" + s0), True, False), (T.sm0[:, 0:96], a("ONE"), a("DEP" + s1), False, True)],
          ("ONE", "DEP" + s0, "DEP" + s1), ("#sm0",), 192)
        V(lambda: v.tensor_reduce(a("CNT" + n), T.sm0[:, 0:96], AxisListType.X, OP.add), ("#sm0",), ("CNT" + n,), 96)
        V(lambda: v.tensor_copy(a("CN" + n), a("CNT" + n)), ("CNT" + n,), ("CN" + n,), 1)
        V(lambda: ts(a("CM" + n), a("CN" + n), 31, None, OP.bitwise_and), ("CN" + n,), ("CM" + n,), 1)
        V(lambda: v.tensor_tensor(a("THC" + n), a("CM" + n), a("THF", 0, 1), OP.add), ("CM" + n, "THF"), ("THC" + n,), 1)

    def far(t, s, ch, ext, lhs, lkey):
        for b in range(3):
            bank = "bg%d_%d" % (ch, (b + (ext[1] == "Y")) % 2)
            x = (512 * b, 512 * b + 512)
            if (ext[1], b) in FARV:
                P(lambda b=b, x=x, bank=bank: [(T[bank][:, 0:512], a(lhs + s, p=96), a(ext, x[0], x[1], p=96), True, True)], (lkey, ext), ("#" + bank,), 512)
                V(lambda x=x, bank=bank: v.tensor_tensor(a("D" + s, *x), a("X" + s, *x), T[bank][:, 0:512], OP.add), ("#" + bank, "X%s.%d" % (s, b)), ("D%s.%d" % (s, b),), 512)
                S(lambda x=x: sc.activation(a("A" + s, *x), a("D" + s, *x), AF.Abs, scale=2048.0), ("D%s.%d" % (s, b),), ("A%s.%d" % (s, b),), 512)
                continue
            P(lambda b=b, x=x, bank=bank: [(T[bank][:, 0:512], a("I128"), a("X" + s, *x), True, False),
                                           (T[bank][:, 0:512], a(lhs + s, p=96), a(ext, x[0], x[1], p=96), False, True)],
              ("I128", "X%s.%d" % (s, b), lkey, ext), ("#" + bank,), 1024)
            S(lambda x=x, bank=bank: sc.activation(a("A" + s, *x), T[bank][:, 0:512], AF.Abs, scale=2048.0), ("#" + bank,), ("A%s.%d" % (s, b),), 512)

    def truth(t, ch):
        s = "%d%d" % (t % 2, ch)
        sm, sk = T["sm%d" % ch], "#sm%d" % ch
        e = "0" if t == 0 else "1"
        cs = "a" if t == 0 else "b"
        vf, vkey, vl, lkey, yb, ykey, up, ukey = state[(t, ch)]
        P(lambda: [(sm[0:96, 0:128], a("S1" + s, 15, 1536, 16), a("I128"), True, False), (sm[0:96, 0:128], a("S2" + s, 15, 1536, 16), a("I128"), False, False),
                   (sm[0:96, 0:128], a("CA"), a("CB"), False, True)], b3("S1" + s) + b3("S2" + s) + ("I128", "CA", "CB"), (sk,), 384)
        V(lambda: ts(a("MT" + s, p=96), sm[0:96, 0:128], float(1.5 * 2 ** 24), float(-1.5 * 2 ** 24), OP.add, OP.add), (sk,), ("MT" + s,), 128)
        far(t, s, ch, "EM" + e, "MT", "MT" + s)
        P(lambda: [(sm[:, 0:96], a("PEN"), a("DEP" + s), True, False), (sm[:, 0:96], a("I128"), a("C1" + cs), False, False), (sm[:, 0:96], a("I128"), a("C2" + cs), False, False)],
          ("PEN", "DEP" + s, "I128", "C1" + cs, "C2" + cs), (sk,), 288)
        P(lambda: [(sm[:, 0:96], a("SUM", 128 * l, 128 * l + 128), sl("A" + s, t, l), False, l == 15) for l in range(16)],
          fam["SUM"] + b3("A" + s), (sk,), 1536)
        V(lambda: v.tensor_tensor_scan(a("M" + s), a("RMN", 0, 96), sm[:, 0:96], 0.0, OP.add, OP.min), (sk, "RMN"), ("M" + s,), 96)
        V(lambda: v.tensor_copy(a("I1" + s, 0, 6), a("M" + s, 15, 96, 16)), ("M" + s,), ("I1" + s,), 6)
        V(lambda: ts(a("I2" + s, 0, 6), a("I1" + s, 0, 6), 2047, None, OP.bitwise_and), ("I1" + s,), ("I2" + s,), 6)
        V(lambda: v.tensor_copy(a("YL" + s, 0, 6), a("I2" + s, 0, 6)), ("I2" + s,), ("YL" + s,), 6)
        add("V", lambda: v.tensor_copy(a("YG" + s), a("X" + s).indirect(a("YL" + s, 0, 6))), b3("X" + s) + ("YL" + s,), ("YG" + s,), 0.2)
        P(lambda: [(sm[0:96, 0:128], a("YG" + s), a("I128"), True, True)], ("YG" + s, "I128"), (sk,), 128)
        S(lambda: sc.activation(a("YT" + s, p=96), sm[0:96, 0:128], AF.Copy, scale=2.0), (sk,), ("YT" + s,), 128)
        far(t, s, ch, "EY" + e, "YT", "YT" + s)
        P(lambda: [(sm[:, 0:96], a("YT" + s, p=96), a("PERM", p=96), True, False), (sm[:, 0:96], a("I128"), a("H96"), False, True)],
          ("YT" + s, "PERM", "I128", "H96"), (sk,), 192)
        V(lambda: v.tensor_tensor(a("YS" + s), yb, sm[:, 0:96], OP.subtract), (ykey, sk), ("YS" + s,), 96)
        ob, ok = T["outy%d_%d" % (t + 1, ch)], "outy%d_%d" % (t + 1, ch)
        V(lambda: ts(ob[:], a("YS" + s), float(1.5 * 2 ** 24), float(-1.5 * 2 ** 24), OP.add, OP.add), ("YS" + s,), (ok,), 96)
        leave("y", t, ch)

    def leave(x, t, ch):
        ob, ok = T["out%s%d_%d" % (x, t + 1, ch)], "out%s%d_%d" % (x, t + 1, ch)
        way = route(T, topo, rank, t + 1, ch)
        b, arr = "in%s%d_%d" % (x, t + 1, ch), "arr%s%d_%d" % (x, t + 1, ch)
        n = len(topo.engines(core, way[1]))
        add("G", lambda: send(g, T, topo, core, way[1], T[b][:], ob[:], arr), (ok,), ("sent%s%d_%d" % (x, t, ch),), 0.5, 6.0, kind="send", sent=n)
        prev = (rank - (STEP if t + 1 < NV else -STEP * (NV - 1))) % len(T.cores)
        back = route(T, topo, prev, t + 1, ch)
        add("R%s%d%d" % (x, t, ch), None, ("sent%s%d_%d" % (x, t, ch),), (b,), 0.0, 0.0, kind="recv", tok=(arr, len(topo.engines(back[-2], core))))

    def asks(t, ch):
        s = "%d%d" % (t % 2, ch)
        sm, sk = T["sm%d" % ch], "#sm%d" % ch
        cs = "a" if t == 0 else "b"
        P(lambda: [(sm[:, 0:96], a("I128"), a("N1" + cs), True, False), (sm[:, 0:96], a("I128"), a("N2" + cs), False, False)],
          ("I128", "N1" + cs, "N2" + cs), (sk,), 192)
        P(lambda: [(sm[:, 0:96], a("SUM", 128 * l, 128 * l + 128), sl("A" + s, t, l), False, l == 15) for l in range(16)],
          fam["SUM"] + b3("A" + s), (sk,), 1536)
        V(lambda: v.tensor_tensor_scan(a("MM" + s, 0, 96), a("RMX", 0, 96), sm[:, 0:96], 0.0, OP.add, OP.max), (sk, "RMX"), ("M1" + s,), 96)
        V(lambda: v.tensor_tensor(a("W" + s, 1, 96), a("MM" + s, 0, 95), sm[:, 1:96], OP.min), (sk, "M1" + s), ("W" + s,), 96)
        V(lambda: v.tensor_tensor_scan(a("MM" + s, 97, 192), a("RMX", 0, 95), a("W" + s, 1, 96), 0.0, OP.add, OP.max), ("W" + s, "RMX"), ("M2" + s,), 96)
        V(lambda: v.tensor_copy(a("E1" + s, 0, 12), a("MM" + s, 15, 192, 16)), ("M1" + s, "M2" + s), ("E1" + s,), 12)
        V(lambda: ts(a("E2" + s, 0, 12), a("E1" + s, 0, 12), 2047, None, OP.bitwise_and), ("E1" + s,), ("E2" + s,), 12)
        V(lambda: ts(a("AB" + s, 0, 12), a("E2" + s, 0, 12), -1, 2047, OP.mult, OP.add), ("E2" + s,), ("AB" + s,), 12)
        add("V", lambda: v.tensor_copy(a("G" + s), a("PR" + s).indirect(a("AB" + s, 0, 12))), b3("PR" + s) + ("AB" + s,), ("G" + s,), 0.4)
        V(lambda: ts(a("ASK" + s, 0, 6), a("MM" + s, 96 + 15, 192, 16), a("TH2"), None, OP.is_ge), ("M2" + s, "TH2"), ("ASK" + s,), 6)
        V(lambda: v.tensor_tensor(a("AW" + s, 0, 6), a("ASK" + s, 0, 6), a("WCOL", 0, 6), OP.mult), ("ASK" + s, "WCOL"), ("AW" + s,), 12)
        P(lambda: [(sm[:, 0:96], a("BV"), a("G" + s, 96, 192), True, True)] +
          [(sm[:, 128:224], a("MVA"), a("G" + s, 0, 96), True, False), (sm[:, 128:224], a("MVB"), a("G" + s, 96, 192), False, True)],
          ("BV", "G" + s, "MVA", "MVB"), (sk,), 288)
        V(lambda: v.tensor_tensor(a("SD" + s), a("D96"), sm[:, 0:96], OP.mult), D96 + (sk,), ("SD" + s,), 96)
        V(lambda: v.tensor_tensor_scan(a("S12" + s), a("HOLD"), a("SD" + s), 0.0, OP.mult, OP.add), ("SD" + s, "HOLD"), ("S12" + s,), 96)
        for c in range(6):
            V(lambda c=c: ts(a("EE" + s, 96 * c, 96 * c + 96), sm[:, 0:96], a("S12" + s, 16 * c + 15, 16 * c + 16), a("AW" + s, c, c + 1), OP.is_equal, OP.mult),
              (sk, "S12" + s, "AW" + s), ("EE%s.%d" % (s, c),), 96)
        S(lambda: sc.activation(a("DAT" + s), sm[:, 128:224], AF.Copy), (sk,), ("DAT" + s,), 96)
        P(lambda: [(sm[:, 0:96], a("BD"), a("EE" + s, 96 * c, 96 * c + 96), c == 0, c == 5) for c in range(6)],
          ("BD",) + tuple("EE%s.%d" % (s, c) for c in range(6)), (sk,), 576)
        V(lambda: v.tensor_tensor(a("LS" + s, 0, 6), a("S12" + s, 15, 96, 16), a("DMP", 0, 6), OP.subtract), ("S12" + s, "DMP"), ("LS" + s,), 12)
        V(lambda: v.tensor_tensor(a("TT" + s, 0, 6), a("LS" + s, 0, 6), a("ASK" + s, 0, 6), OP.mult), ("LS" + s, "ASK" + s), ("TT" + s,), 12)
        V(lambda: v.tensor_tensor(a("R" + s), a("DW"), sm[:, 0:96], OP.mult), DW + (sk,), ("R" + s,), 96)
        V(lambda: v.tensor_tensor_scan(a("RS" + s), a("HOLD"), a("R" + s), 0.0, OP.mult, OP.max), ("R" + s, "HOLD"), ("RS" + s,), 96)
        V(lambda: ts(a("WN" + s, 0, 6), a("RS" + s, 15, 96, 16), 2.5, None, OP.is_lt), ("RS" + s,), ("WN" + s,), 6)
        V(lambda: v.tensor_tensor(a("L2" + s, 0, 6), a("WN" + s, 0, 6), a("TT" + s, 0, 6), OP.mult), ("WN" + s, "TT" + s), ("L2" + s,), 12)
        V(lambda: v.tensor_tensor(a("RS" + s, 0, 6), a("L2" + s, 0, 6), a("DMP", 0, 6), OP.add), ("L2" + s, "DMP"), ("RS" + s,), 12)
        V(lambda: v.tensor_copy(a("SL" + s, 0, 6), a("RS" + s, 0, 6)), ("RS" + s,), ("SL" + s,), 6)
        add("V", lambda: v.tensor_copy(T.tab[:].indirect(a("SL" + s, 0, 6)), a("DAT" + s)), ("SL" + s, "DAT" + s) + tuple(rows), ("tab",), 0.4)

    def both(stage, t):
        for ch in (1, 0):
            now[0] = ch
            r = stage(t, ch)
            if stage == pre:
                state[(t, ch)] = r
        now[0] = 0

    both(pre, 0)
    for t in range(NV):
        both(parents, t)
        both(dependent, t)
        if t < NV - 1:
            counter(t)
        both(names_leave, t)
        both(truth, t)
        both(asks, t)
        if t < NV - 1:
            both(pre, t + 1)
    for ch in (1, 0):
        bv, by, lo = "inv%d_%d" % (NV, ch), "iny%d_%d" % (NV, ch), NC * ch
        V(lambda bv=bv, ch=ch: v.tensor_copy(T["yv_s%d" % ch][:], T[bv][:]), (bv,), ("yvs%d" % ch,), 96)
        V(lambda by=by, ch=ch: ts(T["ye_s%d" % ch][:], T[by][:], 0.5, None, OP.mult), (by,), ("yes%d" % ch,), 96)
        dma(lambda ch=ch, lo=lo: g.sync.dma_start(T.yv[:, lo:lo + NC], T["yv_s%d" % ch][:]), ("yvs%d" % ch,), ("yv%d" % ch,))
        dma(lambda ch=ch, lo=lo: g.sync.dma_start(T.ye[:, lo:lo + NC], T["ye_s%d" % ch][:]), ("yes%d" % ch,), ("ye%d" % ch,))
    P(lambda: [(T.bg0_0[:, 0:256], a("PEX", 128 * c, 128 * c + 128), T.tab[:, 256 * c:256 * c + 256], c == 0, c == 15) for c in range(16)],
      fam["PEX"] + ("tab",), ("#bg0_0",), 4096)
    V(lambda: v.tensor_copy(a("YPF"), T.bg0_0[:, 0:256]), ("#bg0_0",), ("YPF",), 256)
    dma(lambda: g.sync.dma_start(T.yp[:], a("YPF")), ("YPF",), ("yp",))
    return ops
